import numpy as np, ml_dtypes
CORES = [242,247,114,119]
N = 4
BF = ml_dtypes.bfloat16
def gentries(a):
    return np.ascontiguousarray(a.reshape(8, 16, -1).transpose(0, 2, 1)).reshape(8, -1)
def gtable(e):
    e = np.asarray(e); return np.ascontiguousarray(e.reshape(8, -1, 16).transpose(0, 2, 1)).reshape(128, -1).astype(np.int32)
def f(rng, *shape):
    return (rng.standard_normal(shape, dtype=np.float32) * np.exp2(rng.integers(-2, 3, shape[:-1] + (1,)))).astype(BF)
def wide(rng, *shape):
    v = f(rng, *shape).astype(np.float32); k = shape[:-2] + (1, shape[-1])
    return (v * np.exp2(rng.integers(-6, 7, k)) * (rng.random(k) > 0.0625)).astype(BF)
V, W, G, P, Q, RO = 1024, 2048, 256, 256, 128, 4
M = V + (N - 1) * G + 1
def nodes(an, of):
    A = np.full((N, 8, M), M - 1, np.int64); A[..., :V] = an
    O = np.zeros((N, 8, M), np.int64); O[..., :M - 1] = of
    return A, O
def dates(A, O):
    s, p = O, A
    for i in range(3):
        s = s + np.take_along_axis(s, p, 2); p = np.take_along_axis(p, p, 2)
    return s & (W - 1)
def parts(rng):
    u = rng.random((N, 8, V))
    an = np.where(u < 0.25, M - 1, np.where(u < 0.4, rng.integers(V, M - 1, (N, 8, V)), rng.integers(0, V, (N, 8, V))))
    return an, rng.integers(0, W, (N, 8, M - 1)), rng.integers(0, 256, (N, 8, 16, W)), rng.integers(0, V, (N, 8, (N - 1) * G))
def statures(rng):
    sc = np.exp2(rng.integers(-2, 3, (1, 8, 16, 1)).astype(np.float64)); sh = rng.choice(np.array([-0.8, -0.5, -0.2, 0.1]), (N, 8, 1, 1))
    x = rng.standard_normal((N, 8, 16, V)) + 0.7 * rng.standard_normal((N, 8, 1, V)) + sh
    s = rng.standard_normal((N, 8, 16, W)) + 0.7 * rng.standard_normal((N, 8, 1, W))
    return np.floor(8 * x) * 0.125 * sc, np.floor(8 * s) * 0.125 * sc
def pack(x, an, of, s, wk, snd):
    b = lambda v: np.ascontiguousarray(v).reshape(N, 128, -1).astype(np.float32).astype(BF)
    return {"x": b(x), "an0": np.stack([gtable(e) for e in an]), "of0": np.stack([gtable(e) for e in of]), "s0": b(s), "wk": b(wk), "snd": np.stack([gtable(e) for e in snd])}
def setup_inputs(rng):
    an, of, wk, snd = parts(rng); x, s = statures(rng)
    return pack(x, an, of, s, wk, snd)
def setup_inputs_room(rng):
    an, of, wk, snd = parts(rng); day = np.arange(W)
    an[..., 0] = M - 1; an[..., V - 1] = M - 1; of[..., 0] = 0; of[..., V - 1] = W - 2
    D = dates(*nodes(an, of))[..., :V]
    s = rng.integers(36, 61, (N, 8, 16, W)) * 0.25
    s[..., day % 4 == 3] = rng.integers(4, 29, (N, 8, 16, W // 4)) * 0.25
    o = s[1::2]; o[..., day % 4 == 1] = rng.integers(-32, -3, (o.shape[0], 8, 16, W // 4)) * 0.25
    k = rng.permutation(16)
    wk[:, :, k[0]] = 4 * rng.integers(0, 64, (N, 8, W)) + (day + 1) % 4
    wk[1::2, :, k[1]] = 4 * rng.integers(0, 64, (o.shape[0], 8, W)) + (day + 3) % 4
    x = 16 + rng.integers(0, 33, (N, 8, 16, V)) * 0.25
    for q in range(N):
        for g in range(8):
            n = int(rng.choice(np.array([0, 1, 2, P - 1, P, P + 1, P + Q]))); nf = int(rng.choice(np.array([0, 1, Q - 1, Q, Q + 1, P])))
            if q == 0: n = (P, P + 1, P - 1, 1, 0, P, P, P)[g]; nf = (Q, Q + 1, Q - 1, 1, 0, 0, P, Q + 1)[g]
            e = np.flatnonzero(D[q, g] % 2 == 0); e = e[(e > 0) & (e < V - 1)]
            w = np.concatenate([np.array([0, V - 1]), rng.permutation(e)])[:n]
            x[q, g][:, w] = rng.integers(29, 36, (16, len(w))) * 0.25
            i = w[len(w) - min(nf, len(w)):]
            x[q, g][:, i] = rng.integers(0, 4, (16, len(i))) * 0.25
    return pack(x, an, of, s, wk, snd)
def setup_inputs_ties(rng):
    an, of, wk, snd = parts(rng)
    of = rng.choice(np.array([0, 1, W - 1, W // 2, 14]), (N, 8, M - 1)); wk[:, ::2] = rng.choice(np.array([0, 1, 2, 255]), (N, 4, 16, W))
    x = np.floor(4 * rng.random((N, 8, 16, V)) * (0.3 + 0.7 * rng.random((N, 8, 1, V))))
    s = np.floor(4 * rng.random((N, 8, 16, W)) * (0.3 + 0.7 * rng.random((N, 8, 1, W)))) + 2 * (rng.random((N, 8, 1, W)) < 0.4)
    x[..., 0] = -1; x[..., V - 1] = -1
    x = np.where((x == 0) & (rng.random(x.shape) < 0.5), -0.0, x); s = np.where((s == 0) & (rng.random(s.shape) < 0.5), -0.0, s)
    return pack(x, an, of, s, wk, snd)
def setup_inputs_chains(rng):
    an, of, wk, snd = parts(rng); x, s = statures(rng); v = np.arange(V); d = int(rng.integers(0, W))
    for q in range(N):
        for g in range(8):
            k = (g + q) % 8
            if k == 0: an[q, g] = (v + 1) % V
            if k == 1: an[q, g] = v
            if k == 2: an[q, g] = rng.integers(V, M - 1, V)
            if k == 3: an[q, g] = M - 1
            if k == 4: an[q, g] = rng.choice(np.array([0, 5, V - 1]), V)
            if k == 5: an[q, g] = np.where(v == 0, M - 1, v - 1)
            if k > 5:
                an[q, g] = M - 1; of[q, g, :V] = d
                w = 1 + rng.permutation(255)[:16]; wk[q, g, :, d] = w; c = (d + 7 * w) & (W - 1)
                i = np.sort(rng.permutation(16)[:2])
                s[q, g] = 16 + 0.25 * rng.integers(0, 32, (16, W))
                s[q, g][:, c[i[0]]] = 0.25 * rng.integers(0, 16, 16)
                m = np.arange(P) if k == 6 else np.arange(int(rng.integers(0, 16)), V, 16)
                y = 28 + 0.25 * rng.integers(0, 16, (16, V))
                y[:, m] = 8 + 0.25 * rng.integers(0, 16, (16, len(m)))
                if k == 6: y[:, rng.permutation(P)[:56]] = -8 + 0.25 * rng.integers(0, 16, (16, 56))
                if k == 7: s[q, g][:, c[i[1]]] = -16 + 0.25 * rng.integers(0, 16, 16)
                x[q, g] = y
    snd[:, ::2] = rng.choice(np.array([0, 3, V // 2, V - 1]), (N, 4, (N - 1) * G))
    return pack(x, an, of, s, wk, snd)
def setup_inputs_calm(rng):
    an, of, wk, snd = parts(rng); x, s = statures(rng); q = int(rng.integers(0, N)); g = int(rng.integers(0, 8))
    x[:, g] += 64
    x[(q + 2) % N] += 64; x[q] = np.minimum(x[q], 20) - 64
    o = s[(q + 1) % N]; o[..., 1::2] -= 128
    w = rng.permutation(256)[:16]; wk[:, g, :, 0] = w; day = (7 * w) & (W - 1)
    for r in range(N):
        if r != q: s[r, g][:, day] = -2.0 ** 20
    x[q, :, :, 0] = -2.0 ** 20
    return pack(x, an, of, s, wk, snd)
def setup_inputs_spread(rng):
    an, of, wk, snd = parts(rng)
    of = np.minimum(np.exp2(13 * rng.random((N, 8, M - 1))).astype(np.int64) - 1, W - 1)
    x = np.abs(wide(rng, N, 8, 16, V).astype(np.float32)); s = np.abs(wide(rng, N, 8, 16, W).astype(np.float32))
    k = rng.permutation(8); sc = np.ones((1, 8, 1, 1), np.float32); sc[:, k[0]] = 2.0 ** -40; sc[:, k[1]] = 512
    x = np.minimum(x * sc, np.float32(2.0 ** 20)); s = np.minimum(s * sc, np.float32(2.0 ** 20))
    x[:, k[1], :, V - 1] = 2.0 ** 20; s[:, k[1], :, W - 1] = 2.0 ** 20
    return pack(x, an, of, s, wk, snd)
def check_inputs(d):
    bad = []
    for k, lo, hi in (("x", -2 ** 20, 2 ** 20), ("s0", -2 ** 20, 2 ** 20), ("wk", 0, 255), ("an0", 0, M - 1), ("of0", 0, W - 1), ("snd", 0, V - 1)):
        v = np.asarray(d[k]).astype(np.float64)
        if not (np.min(v) >= lo and np.max(v) <= hi): bad.append("range of " + k)
        elif k == "wk" and np.any(v != np.floor(v)): bad.append("whole numbers of wk")
        elif k in ("x", "s0") and np.any((v != 0) & (np.abs(v) < 2.0 ** -100)): bad.append("tiny numbers of " + k)
    return bad
def best(S, K, x, D):
    c = (D + 7 * K[:, D]) & (W - 1)
    e = np.sum((x[:, None, :] > S[:, c]).astype(np.int64), axis=0)
    k = np.argmax(e, axis=0); i = np.arange(len(D))
    return c[k, i], e[k, i]
def put(S, c, x):
    u, i = np.unique(c, return_index=True)
    S[:, u] = x[:, i]
def reference(x, an0, of0, s0, wk, snd):
    X = x.astype(np.float32).reshape(N, 8, 16, V); S = s0.astype(np.float32).reshape(N, 8, 16, W).copy(); K = wk.astype(np.float32).astype(np.int64).reshape(N, 8, 16, W)
    A, O = nodes(np.stack([gentries(e) for e in an0]).astype(np.int64), np.stack([gentries(e) for e in of0]).astype(np.int64))
    sl = np.stack([gentries(e) for e in snd]).astype(np.int64).reshape(N, 8, N - 1, G)
    odd = np.zeros(N, np.int64)
    for t in range(RO):
        D = dates(A, O)[..., :V]
        a = np.sum((X >= np.take_along_axis(S, D[:, :, None, :], 3)).astype(np.int64), axis=2)
        moves = np.zeros(N, np.int64); go = {}
        for q in range(N):
            for g in range(8):
                v = np.flatnonzero(a[q, g] < 5)[:P]
                c, e = best(S[q, g], K[q, g], X[q, g][:, v], D[q, g, v])
                ok = e >= 9 + odd[q]; w = v[ok]
                A[q, g, w] = M - 1; O[q, g, w] = c[ok]
                put(S[q, g], c[ok], X[q, g][:, w])
                moves[q] += len(w)
                r = v[~ok][:Q]; go[q, g] = (X[q, g][:, r], D[q, g, r])
        for q in range(N):
            for g in range(8):
                y, b = go[(q - 1 - t % (N - 1)) % N, g]
                c, e = best(S[q, g], K[q, g], y, b)
                ok = e >= 9 + odd[q]
                put(S[q, g], c[ok], y[:, ok])
        odd = moves & 1
        for q in range(N):
            for d in range(1, N):
                p = (q - d) % N
                O[q, :, V + (d - 1) * G:V + d * G] = np.take_along_axis(D[p], sl[p, :, d - 1], 1)
    return {"ys": S.reshape(N, 128, W).astype(BF), "yan": A[..., :V].astype(np.float32), "yof": O[..., :V].astype(np.float32)}

@@ -1,0 +1,477 @@
+from concourse.mybir import AluOpType as A, ActivationFunctionType as AF, AxisListType as AX
+
+FLAG = 262144.0
+BIG = 65536.0
+LOW = -1073741824.0
+RO = 4
+F, B, H, I, U = "float32", "bfloat16", "float16", "int32", "uint16"
+SB = {
+    "anI": (64, I), "ofI": (112, I), "snI": (48, I), "wkb": (2048, B), "xw": (1040, B), "sd": (2320, B),
+    "pI": (3, I), "pp": (3, F), "tc": (8, F), "lmc": (16, F), "n512": (512, I), "kI": (256, I), "m4": (128, I),
+    "id16": (128, H), "idb": (128, B), "idF": (128, F), "jF": (128, F), "j16": (128, H), "upr": (128, B),
+    "one": (128, B), "seven": (128, B), "gb16": (128, H), "gi16": (8, H), "gib": (8, B), "gik": (8, B), "pm0": (256, F), "pm1": (256, F), "pmg": (128, F),
+    "mk": (256, H), "mkg": (256, H), "lane": (256, B), "ct8": (128, B), "selh": (2048, H), "selb": (2048, B), "selF": (2048, F),
+    "ex": (16, U), "exg": (16, U), "ex8": (8, U), "dgt": (6, U), "v1c": (16, F), "smI": (1024, I), "smk": (1024, B), "du": (32, F), "lo16": (512, H),
+    "an1": (64, F), "ofE": (1792, H), "pw": (1800, F), "p2w": (1800, F), "rf16": (1024, H), "w1": (2064, F), "w2": (1800, F), "w3": (1800, F), "t8": (1032, F),
+    "fl": (1024, B), "wd": (1024, F), "p1h": (64, H), "p2h": (64, H), "p3h": (64, H), "l1": (64, U), "l2": (64, U), "l3": (64, U), "sl": (48, U), "cw": (2056, F), "cq": (2048, F),
+    "ldI": (64, I), "lfd": (64, U), "cv": (1032, F), "cmp": (4096, B), "xr": (4096, B), "bz": (120, B), "rz": (24, B), "rkI": (64, I), "loI": (64, I), "hiI": (16, I),
+    "oa": (1024, H), "ob": (128, H), "th": (1088, B), "win": (144, F), "wg": (128, F), "g1": (16, F), "lv": (16, U), "lvf": (16, F), "nb": (8, F), "vld": (16, F),
+    "xg": (272, B), "cg": (256, U), "cgf": (256, F), "dbf": (256, F), "dbi": (264, I), "kb": (128, F), "ka": (128, F), "ks": (112, F), "sm": (128, F), "smi": (64, I), "u16s": (64, U),
+    "rdb": (2, B), "thr": (4, F), "xe": (256, H), "xf": (256, F), "rr": (256, H), "wv": (256, F), "eq": (2048, B), "scn": (2048, B), "gl": (16, U), "dgh": (128, H), "yb": (384, F),
+    "ghs": (2304, F), "ghl": (2304, F), "gxs": (512, B), "gxl": (512, B), "gds": (64, U), "gdl": (64, U),
+}
+SCRATCH = {k: ("sbuf", [128, n], d) for k, (n, d) in SB.items()}
+SCRATCH.update({"ck": ("sbuf", [1, 256], B), "ckg": ("sbuf", [1, 128], B), "cb": ("sbuf", [1, 2048], B)})
+PS = ("pA", "pB", "pC", "pD", "pE", "pF", "pG", "pH")
+SCRATCH.update({k: ("psum", [128, 512], F) for k in PS})
+SEMAPHORES = ["qV", "qS", "qP", "qG", "ls"] + ["d%d" % i for i in range(11)] + ["gh%d" % t for t in range(3)] + ["gx%d" % t for t in range(RO)] + ["gd%d" % t for t in range(RO)]
+
+
+def layer(g, T):
+    eng = {"V": g.vector, "S": g.scalar, "P": g.tensor, "G": g, "Y": g.sync}
+    cnt = {"V": 0, "S": 0, "P": 0, "G": 0}
+    seen = {q: {} for q in eng}
+    hist = {}
+    dma = [0]
+
+    def reg(r):
+        return (r, 0, 1 << 20) if isinstance(r, str) else r
+
+    def prepare(q, reads, writes):
+        best = {}
+        for rs, w in ((reads, False), (writes, True)):
+            for r in rs:
+                name, lo, hi = reg(r)
+                for e in hist.get(name, ()):
+                    other = e[3] != q
+                    bank = name in PS and other
+                    if not (lo < e[1] and e[0] < hi) and not bank:
+                        continue
+                    if not (w or e[2] or bank) or (q == "P" and not other and name in PS):
+                        continue
+                    if seen[q].get(e[4], 0) < e[5] and (e[4] not in best or best[e[4]][5] < e[5]):
+                        best[e[4]] = e
+        for s in best:
+            e = best[s]
+            if not any(o != s and best[o][6].get(s, 0) >= e[5] for o in best):
+                eng[q].wait_ge(T.sem[s], e[5])
+        for e in best.values():
+            for s, n in list(e[6].items()) + [(e[4], e[5])]:
+                if seen[q].get(s, 0) < n:
+                    seen[q][s] = n
+
+    def record(q, sem, count, reads, writes):
+        clock = dict(seen[q[0]])
+        for rs, w in ((reads, False), (writes, True)):
+            for r in rs:
+                name, lo, hi = reg(r)
+                h = hist.setdefault(name, [])
+                h[:] = [e for e in h if not (lo <= e[0] and e[1] <= hi and (w or (e[3] == q and not e[2])))]
+                h.append((lo, hi, w, q, sem, count, clock))
+
+    def op(q, fns, reads, writes):
+        prepare(q, reads, writes)
+        for f in fns if isinstance(fns, list) else [fns]:
+            f().then_inc(T.sem["q" + q], 1)
+            cnt[q] += 1
+        record(q, "q" + q, cnt[q], reads, writes)
+
+    def copy(q, out, in_, reads, writes):
+        prepare(q, reads, writes)
+        sem = "d%d" % dma[0]
+        dma[0] += 1
+        eng[q].dma_start(out, in_).then_inc(T.sem[sem], 16)
+        record(q + "*", sem, 16, reads, writes)
+
+    def landed(region, sem, count):
+        hist.setdefault(region[0], []).append((region[1], region[2], True, "net", sem, count, {}))
+
+    def finish(extra):
+        for q in cnt:
+            if cnt[q]:
+                g.wait_ge(T.sem["q" + q], cnt[q])
+        for i in range(dma[0]):
+            g.wait_ge(T.sem["d%d" % i], 16)
+        for s, n in extra:
+            g.wait_ge(T.sem[s], n)
+
+    return op, copy, landed, prepare, finish
+
+
+def alternate(a, b):
+    for i in range(max(len(a), len(b))):
+        for c in (a, b):
+            if i < len(c):
+                c[i]()
+
+
+def rank_program(g, core, T, topo):
+    rank = T.rank_of(core)
+    if rank is None:
+        return
+    cores = T.cores
+    N = len(cores)
+    op, copy, landed, prepare, finish = layer(g, T)
+    V, S, P = g.vector, g.scalar, g.tensor
+    sent = [0]
+
+    def v(f, r, w):
+        op("V", f, r, w)
+
+    def s(f, r, w):
+        op("S", f, r, w)
+
+    def p(f, r, w):
+        op("P", f, r, w)
+
+    def tc(o, i):
+        return lambda: V.tensor_copy(o, i)
+
+    def tt(o, a, b, f):
+        return lambda: V.tensor_tensor(o, a, b, f)
+
+    def ts(o, a, s1, f1, s2=None, f2=None):
+        if f2 is None:
+            return lambda: V.tensor_scalar(o, a, s1, None, f1)
+        return lambda: V.tensor_scalar(o, a, s1, s2, f1, f2)
+
+    def ms(o, c):
+        return lambda: V.memset(o, c)
+
+    def act(o, i, f=AF.Copy, bias=0.0, scale=1.0):
+        return lambda: S.activation(o, i, f, bias=bias, scale=scale)
+
+    def mm(o, l, r, st=True, sp=True):
+        return lambda: P.matmul(o, l, r, st, sp)
+
+    def send(dst, out, in_, reads, sem):
+        d = cores[dst]
+        prepare("G", reads, [])
+        rid, pid = topo.addr(d, core)
+        g.remote_dma(out, in_, T.sem[sem], T.sem.ls, pid, rid, topo.mask(core, d))
+        sent[0] += len(topo.engines(core, d))
+
+    def iota(name, view, pat, base, ch, fl=False):
+        if fl:
+            op("G", lambda: g.iota(view, pat, base, ch, allow_small_or_imprecise_dtypes=True), [], [name])
+        else:
+            op("G", lambda: g.iota(view, pat, base, ch), [], [name])
+
+    v([ms(T.xw[:, 0:1], LOW), ms(T.sd[:, 0:1], 0.0)], [], [("xw", 0, 16), ("sd", 0, 16)])
+    copy("Y", T.anI[:], T.an0[:], [], ["anI"])
+    copy("Y", T.ofI[:], T.of0[:], [], ["ofI"])
+    copy("S", T.wkb[:], T.wk[:], [], ["wkb"])
+    copy("Y", T.sd[:, 1:2049], T.s0[:], [], [("sd", 1, 2049)])
+    copy("Y", T.xw[:, 1:1025], T.x[:], [], [("xw", 1, 1025)])
+    copy("Y", T.snI[:], T.snd[:], [], ["snI"])
+    iota("pI", T.pI[:, 0:1], [[0, 1]], 0, 1)
+    iota("n512", T.n512[:], [[1, 512]], 0, 0)
+    iota("v1c", T.v1c[:, 0:8], [[128, 8]], 1, 1, True)
+    iota("ct8", T.ct8[:], [[0, 16], [1, 8]], -256, 0, True)
+    iota("ck", T.ck[:], [[-4096, 16], [0, 16]], 61440, 0, True)
+    iota("ckg", T.ckg[:], [[-4096, 16], [0, 8]], 61440, 0, True)
+    iota("du", T.du[:, 0:16], [[16, 16]], 2056, 0, True)
+    iota("smI", T.smI[:], [[16, 8], [1, 128]], 0, 0)
+
+    P15, P4, PC = T.pp[:, 0:1], T.pp[:, 1:2], T.pp[:, 2:3]
+    v(ms(T.one[:], 1.0), [], ["one"])
+    v([ts(T.pI[:, 1:2], T.pI[:, 0:1], 15, A.bitwise_and), ts(T.pI[:, 2:3], T.pI[:, 0:1], 4, A.arith_shift_right)], ["pI"], ["pI2"])
+    v([tc(P15, T.pI[:, 1:2]), tc(P4, T.pI[:, 2:3]), tc(PC, T.pI[:, 0:1])], ["pI", "pI2"], ["pp"])
+    v([ts(T.lmc[:], T.n512[:, 0:16], P15, A.is_equal), ts(T.m4[:], T.n512[:, 0:128], 4, A.arith_shift_right), ts(T.kI[:], T.n512[:, 0:256], 15, A.bitwise_and)], ["n512", "pp"], ["lmc", "m4", "kI"])
+    v(ts(T.an1[:], T.anI[:], 1.0, A.add), ["anI"], ["an1"])
+    v([ts(T.gb16[:], T.m4[:], P4, A.is_equal), tc(T.l1[:], T.an1[:])], ["m4", "pp", "an1"], ["gb16", "l1"])
+    v([ts(T.rf16[:, k::16], T.an1[:], T.lmc[:, k:k + 1], A.mult) for k in range(16)], ["an1", "lmc"], ["rf16"])
+    p([mm(T.pG[:], T.gb16[:], T.rf16[:, 0:512]), mm(T.pH[:], T.gb16[:], T.rf16[:, 512:1024])], ["gb16", "rf16"], ["pG", "pH"])
+    v([ms(T.pw[:, 1025:1794], 1793.0), ms(T.pw[:, 0:1], 1793.0)], [], [("pw", 1025, 1794), ("pw", 0, 1)])
+    s(act(T.pw[:, 1:513], T.pG[:]), ["pG"], [("pw", 1, 513)])
+    s(act(T.pw[:, 513:1025], T.pH[:]), ["pH"], [("pw", 513, 1025)])
+    v([ts(T.ofE[:, k::16], T.ofI[:], T.lmc[:, k:k + 1], A.mult) for k in range(16)], ["ofI", "lmc"], ["ofE"])
+    OFB = [(bank, 512 * b, min(512 * b + 512, 1792)) for b, bank in enumerate(("pA", "pB", "pC", "pD"))]
+    for bank, lo, hi in OFB:
+        p(mm(T[bank][:, 0:hi - lo], T.gb16[:], T.ofE[:, lo:hi]), ["gb16", "ofE"], [bank])
+    for bank, lo, hi in OFB:
+        s(act(T.w1[:, lo + 1:hi + 1], T[bank][:, 0:hi - lo]), [bank], [("w1", lo + 1, hi + 1)])
+    for bank, lo, hi in OFB[:2]:
+        s(act(T.wd[:, lo:hi], T[bank][:]), [bank], [("wd", lo, hi)])
+    v(ts(T.id16[:], T.n512[:, 0:128], PC, A.is_equal), ["n512", "pp"], ["id16"])
+    v([ms(T.p2w[:, 1025:1794], 1793.0), ms(T.p2w[:, 0:1], 1793.0)], [], [("p2w", 1025, 1794), ("p2w", 0, 1)])
+    v([ts(T.selh[:, 128 * k:128 * k + 128], T.id16[:], T.lmc[:, k:k + 1], A.mult) for k in range(16)], ["id16", "lmc"], ["selh"])
+    v(lambda: V.tensor_copy(T.p2w[:, 1:1025], T.pw[:, 0:1794].indirect(T.l1[:])), ["pw", "l1"], [("p2w", 1, 1025)])
+    v(tc(T.rf16[:], T.p2w[:, 1:1025]), ["p2w"], ["rf16"])
+
+    def conv(src, name, c0, cols, sel, bank, extra=None):
+        o = T[bank][:, 0:cols]
+        fs = [mm(o, T[sel][:, 128 * k:128 * k + 128], src[:, c0 + k:c0 + 16 * cols:16], k == 0, k == 15 and extra is None) for k in range(16)]
+        if extra is not None:
+            fs.append(mm(o, T.id16[:], T[extra][:], False, True))
+        p(fs, [(name, c0, c0 + 16 * cols), sel, "id16"] + ([extra] if extra else []), [bank])
+
+    conv(T.rf16, "rf16", 0, 64, "selh", "pF")
+    zs = [("w1", 1793, 2064), ("w1", 0, 1), ("w2", 1793, 1794), ("w2", 0, 1), ("w3", 1793, 1794), ("w3", 0, 1), ("t8", 0, 1)]
+    v([ms(T[n][:, a:b], 0.0) for n, a, b in zs] + [ms(T.dbi[:, 0:1], 0), ms(T.cv[:, 0:1], 1.0), ms(T.cw[:, 0:1], 1.0), ms(T.xg[:, 0:1], LOW)], [],
+      zs + [("dbi", 0, 1), ("cv", 0, 1), ("cw", 0, 1), ("xg", 0, 1)])
+    for n in ("w2", "w3"):
+        s(act(T[n][:, 1025:1537], T.pC[:]), ["pC"], [(n, 1025, 1537)])
+        s(act(T[n][:, 1537:1793], T.pD[:, 0:256]), ["pD"], [(n, 1537, 1793)])
+    W = ("w1", "w2", "w3")
+    PH = ("p1h", "p2h", "p3h")
+    LL = ("l1", "l2", "l3")
+
+    def addend(l):
+        for h in (0, 1):
+            a = 512 * h
+            s(act(T.wd[:, a:a + 512], T[W[l]][:, 1 + a:513 + a]), [(W[l], 1 + a, 513 + a)], [("wd", a, a + 512)])
+
+    def jump(l, halves=(0, 1)):
+        nm = "t8" if l == 2 else W[l + 1]
+        for h in halves:
+            a = 512 * h
+            v(tt(T[nm][:, a + 1:a + 513], T[W[l]][:, 0:1794].indirect(T[LL[l]][:, 32 * h:32 * h + 32]), T.wd[:, a:a + 512], A.add),
+              [(W[l], 0, 1794), LL[l], ("wd", a, a + 512)], [(nm, a + 1, a + 513)])
+
+    def jumplist(l):
+        for h in (0, 1):
+            a = 512 * h
+            s(act(T.fl[:, a:a + 512], T[W[l]][:, 1 + a:513 + a], AF.Relu, -2048.0, 0.015625), [(W[l], 1 + a, 513 + a)], [("fl", a, a + 512)])
+        conv(T.fl, "fl", 0, 64, "selb", "pF", PH[l])
+        addend(l)
+
+    def jumplist2(l):
+        v(ts(T[LL[l]][:], T.pF[:, 0:64], 1793.0, A.min), ["pF"], [LL[l]])
+
+    v(ts(T.idF[:], T.n512[:, 0:128], PC, A.is_equal), ["n512", "pp"], ["idF"])
+    s([act(T.selF[:, 128 * k:128 * k + 128], T.idF[:], AF.Copy, 0.0, T.lmc[:, k:k + 1]) for k in range(16)], ["idF", "lmc"], ["selF"])
+    v(tc(T.l2[:], T.pF[:, 0:64]), ["pF"], ["l2"])
+    v(tc(T.p2h[:], T.pF[:, 0:64]), ["pF"], ["p2h"])
+    v(lambda: V.tensor_copy(T.rf16[:], T.p2w[:, 0:1794].indirect(T.l2[:])), ["p2w", "l2"], ["rf16"])
+    conv(T.rf16, "rf16", 0, 64, "selh", "pF")
+    jump(0)
+    addend(1)
+    jump(1)
+    addend(2)
+    v(tc(T.l3[:], T.pF[:, 0:64]), ["pF"], ["l3"])
+    v([tc(T.p3h[:], T.pF[:, 0:64]), tc(T.p1h[:], T.an1[:])], ["pF", "an1"], ["p3h", "p1h"])
+    jump(2)
+    conv(T.t8, "t8", 1, 64, "selF", "pG")
+    v(ts(T.sl[:], T.snI[:], 1.0, A.add), ["snI"], ["sl"])
+    N1 = T.n512[:, 0:128]
+    v([ts(T.idb[:], N1, PC, A.is_equal), ts(T.seven[:], N1, PC, A.is_equal, 7.0, A.mult), ts(T.lo16[:], T.n512[:], 1.0, A.add)], ["n512", "pp"], ["idb", "seven", "lo16"])
+    v([ms(T.cb[:, 512 * b:512 * b + 512], 512.0 * b) for b in range(4)], [], ["cb"])
+    G8 = T.n512[:, 0:8]
+    v([ts(T.gib[:], G8, P4, A.is_equal), ts(T.gi16[:], G8, P4, A.is_equal), ts(T.gik[:], G8, P4, A.is_equal, BIG, A.mult)], ["n512", "pp"], ["gib", "gi16", "gik"])
+    CB = list(enumerate(("pH", "pC", "pA", "pB")))
+    for b, bank in CB:
+        c = 512 * b
+        p([mm(T[bank][:], T.seven[:], T.wkb[:, c:c + 512], True, False), mm(T[bank][:], T.id16[:], T.lo16[:], False, False),
+           mm(T[bank][:], T.one[0:1, :], T.cb[:, c:c + 512], False, True)], ["seven", "wkb", "id16", "lo16", "one", "cb"], [bank])
+    v([ts(T.cq[:, 0:128], N1, PC, A.is_equal, -4096.0, A.mult), ts(T.cq[:, 128:256], N1, PC, A.is_gt)], ["n512", "pp"], [("cq", 0, 256)])
+    v(tt(T.upr[:], T.cq[:, 0:128], T.cq[:, 128:256], A.add), [("cq", 0, 256)], ["upr"])
+    v([ms(T.bz[:, 0:56], 0.0), ms(T.rz[:, 0:8], 0.0), ms(T.wg[:, 64:128], 0.0)], [], [("bz", 0, 56), ("rz", 0, 8), ("wg", 64, 128)])
+    v([ts(T.tc[:, 5:6], P4, 17.0, A.mult), ts(T.v1c[:, 8:16], T.v1c[:, 0:8], 0.5, A.mult)], ["pp", "v1c"], ["tcd", "v1c"])
+    v(tt(T.tc[:, 7:8], T.tc[:, 5:6], P15, A.add), ["tcd", "pp"], ["tce"])
+    v([tc(T.dgt[:, 0:1], T.tc[:, 7:8]), ts(T.dgt[:, 2:3], T.tc[:, 7:8], 1.0, A.add), tc(T.ex[:], T.n512[:, 0:16])], ["tce", "n512"], ["dgl", "ex"])
+    for b, bank in CB:
+        c = 512 * b
+        v(ts(T.cq[:, c:c + 512], T[bank][:], 2048.5, A.is_gt, -2048.0, A.mult), [bank], [("cq", c, c + 512)])
+        v(tt(T.cw[:, 1 + c:513 + c], T[bank][:], T.cq[:, c:c + 512], A.add), [bank, ("cq", c, c + 512)], [("cw", 1 + c, 513 + c)])
+
+    def constants2():
+        K1 = T.kI[:, 0:128]
+        v([tc(T.lane[:], T.kI[:]), ts(T.mk[:], T.kI[:], P15, A.is_equal), ts(T.mkg[:, 0:128], K1, 0.0, A.is_ge), ts(T.mkg[:, 128:256], K1, P15, A.is_equal)], ["kI", "pp"], ["lane", "mk", "mkg"])
+        v([ts(T.tc[:, 0:1], P15, 16.0, A.mult), ts(T.tc[:, 1:2], P15, 8.0, A.mult), ts(T.tc[:, 3:4], P4, 8.0, A.mult), ts(T.tc[:, 2:3], P15, 8.0, A.is_ge),
+           ts(T.tc[:, 4:5], P15, -1.0, A.mult, 127.0, A.add), ts(T.smi[:, 0:16], T.n512[:, 0:16], 7, A.bitwise_and)], ["pp", "n512"], ["tc", "smi"])
+        v([tt(T.sm[:, 0:1], T.tc[:, 0:1], P4, A.add), tt(T.sm[:, 1:2], T.tc[:, 1:2], P4, A.add), tt(T.sm[:, 3:4], T.tc[:, 3:4], P15, A.add)], ["tc", "pp"], ["sm"])
+        v([ts(T.sm[:, 2:3], T.sm[:, 0:1], 8.0, A.add), tc(T.dgt[:, 4:5], T.sm[:, 3:4])], ["sm"], ["dg8", "sm2"])
+        v([ts(T.pm0[:], T.n512[:, 0:256], T.sm[:, 0:1], A.is_equal), ts(T.pm1[:], T.n512[:, 0:256], T.sm[:, 2:3], A.is_equal), ts(T.pmg[:], N1, T.sm[:, 1:2], A.is_equal)],
+          ["n512", "sm", "sm2"], ["pm0", "pm1", "pmg"])
+        v([ts(T.j16[:], N1, PC, A.add, 127.0, A.is_equal), ts(T.jF[:], N1, PC, A.add, 127.0, A.is_equal), tc(T.exg[:], T.smi[:, 0:16]), ts(T.ex8[:], G8, 2.0, A.mult, T.tc[:, 2:3], A.add),
+           ts(T.du[:, 0:16], T.du[:, 0:16], P15, A.add)], ["n512", "pp", "smi", "tc", "du"], ["j16", "jF", "exg", "ex8", "du"])
+        v(ts(T.du[:, 16:32], T.du[:, 0:16], -256.0, A.add), ["du"], ["du"])
+        v(ts(T.smk[:], T.smI[:], T.tc[:, 4:5], A.is_gt), ["smI", "tc"], ["smk"])
+        v(ms(T.thr[:, 0:1], 9.0 * BIG), [], ["thr"])
+
+    DUS, DUW = T.du[:, 0:16], T.du[:, 16:32]
+
+    def tree(w):
+        v(tc(T.kb[:, 0:8 * w], T.pD[:, 8 * w:16 * w]), ["pD"], ["kb"])
+        v(tt(T.ka[:, 0:8 * w], T.pD[:, 0:8 * w], T.kb[:, 0:8 * w], A.max), ["pD", "kb"], ["ka"])
+        v(tt(T.kb[:, 0:4 * w], T.ka[:, 0:4 * w], T.ka[:, 4 * w:8 * w], A.max), ["ka"], ["kb"])
+        v(tt(T.ka[:, 0:2 * w], T.kb[:, 0:2 * w], T.kb[:, 2 * w:4 * w], A.max), ["kb"], ["ka"])
+        v(tt(T.ks[:, 0:w], T.ka[:, 0:w], T.ka[:, w:2 * w], A.max), ["ka"], [("ks", 0, 16)])
+        v([ts(T.ks[:, 16:16 + w], T.ks[:, 0:w], T.thr[:, 0:1], A.is_ge), tc(T.smi[:, 0:w], T.ks[:, 0:w])], [("ks", 0, 16), "thr"], [("ks", 16, 32), ("smi", 0, 16)])
+
+    def chosen(w):
+        v(ts(T.smi[:, 16:16 + w], T.smi[:, 0:w], 4095, A.bitwise_and), [("smi", 0, 16)], [("smi", 16, 32)])
+        v(tt(T.ks[:, 48:48 + w], T.smi[:, 16:16 + w], T.ks[:, 16:16 + w], A.mult), [("smi", 16, 32), ("ks", 16, 32)], [("ks", 48, 64)])
+
+    def eqdays(nh):
+        for h in range(nh):
+            v([ts(T.eq[:, b * 128:b * 128 + 128], T.rr[:, 128 * h:128 * h + 128], T.sm[:, 112 + b:113 + b], A.is_equal) for b in range(8 * h, 8 * h + 8)],
+              ["rr", ("sm", 112, 128)], [("eq", 1024 * h, 1024 * h + 1024)])
+
+    def scan(h):
+        a = slice(1024 * h, 1024 * h + 1024)
+        v(lambda: V.tensor_tensor_scan(T.scn[:, a], T.eq[:, a], T.smk[:], 0.0, A.max, A.mult), [("eq", a.start, a.stop), "smk"], [("scn", a.start, a.stop)])
+
+    def dayoffsets(w):
+        return [
+            lambda: v(tt(T.sm[:, 80:80 + w], T.scn[:, 127:128 * w:128], T.du[:, 0:w], A.mult), ["scn", "du"], [("sm", 80, 96)]),
+            lambda: v(tt(T.sm[:, 96:96 + w], T.sm[:, 64:64 + w], T.sm[:, 80:80 + w], A.max), [("sm", 64, 96)], [("sm", 96, 112)]),
+            lambda: v(tc(T.u16s[:, 16:16 + w], T.sm[:, 96:96 + w]), [("sm", 96, 112)], [("u16s", 16, 32)])]
+
+    def copies(q, src, sname, so, dst, n, ks):
+        f = act if q == "S" else tc
+        op(q, [f(T.xr[:, dst + k:dst + 16 * n:16], src[:, so:so + n]) for k in ks], [(sname, so, so + n)], [("xr" + q, dst, dst + 1)])
+
+    for t in range(RO):
+        last = t == RO - 1
+        gxa, gda, gha = (128 * t, 128 * t + 128), (16 * t, 16 * t + 8), (768 * t, 768 * t + 768)
+        to, fro = (rank + 1 + t % (N - 1)) % N, (rank - 1 - t % (N - 1)) % N
+        if not last:
+            s(act(T.ghs[:, gha[0]:gha[1]], T.t8[:, 0:1025].indirect(T.sl[:])), [("t8", 0, 1025), "sl"], [("ghs",) + gha])
+            for d in range(1, N):
+                a = gha[0] + 256 * (d - 1)
+                send((rank + d) % N, T.ghl[:, a:a + 256], T.ghs[:, a:a + 256], [("ghs", a, a + 256)], "gh%d" % t)
+            landed(("ghl",) + gha, "gh%d" % t, sum(len(topo.engines(cores[(rank - d) % N], core)) for d in range(1, N)))
+        v(tc(T.ldI[:], T.pG[:, 0:64]), ["pG"], ["ldI"])
+        v(ts(T.ldI[:], T.ldI[:], 2047, A.bitwise_and), ["ldI"], ["ldI"])
+        v(ts(T.lfd[:], T.ldI[:], 1.0, A.add), ["ldI"], ["lfd"])
+        for h in (0, 1):
+            s(act(T.cv[:, 1 + 512 * h:513 + 512 * h], T.cw[:, 0:2049].indirect(T.lfd[:, 32 * h:32 * h + 32])), ["cw", "lfd"], [("cv", 1 + 512 * h, 513 + 512 * h)])
+            v(tt(T.cmp[:, 512 * h:512 * h + 512], T.sd[:, 0:2049].indirect(T.lfd[:, 32 * h:32 * h + 32]), T.xw[:, 1 + 512 * h:513 + 512 * h], A.is_le),
+              [("sd", 0, 2049), "lfd", ("xw", 1, 1025)], [("cmp", 512 * h, 512 * h + 512)])
+            p([mm(T.pA[:, 8 * c:8 * c + 8], T.cmp[:, 128 * c:128 * c + 128], T.gib[:]) for c in range(4 * h, 4 * h + 4)], [("cmp", 512 * h, 512 * h + 512), "gib"], ["pA"])
+        v(ts(T.bz[:, 56:120], T.pA[:, 0:64], 4.5, A.is_lt), ["pA"], [("bz", 56, 120)])
+        p([mm(T.pB[:, 0:64], T.upr[:], T.bz[:, 56:120], True, False)] + [mm(T.pB[:, 0:64], T.one[:], T.bz[:, 56 - 8 * q:120 - 8 * q], False, q == 7) for q in range(1, 8)],
+          ["upr", "one", "bz"], ["pB"])
+        v(tc(T.rkI[:], T.pB[:, 0:64]), ["pB"], ["rkI"])
+        s([act(T.th[:, c::17], T.pB[:, 0:64], AF.Sign, 16.0 * c - 4096.5, -1.0) for c in range(17)], ["pB"], ["th"])
+        p([mm(T.pH[:, 0:8], T.one[:], T.bz[:, 56 + 8 * c:64 + 8 * c], c == 0, c == 7) for c in range(8)], ["one", "bz"], ["pH"])
+        v(ts(T.loI[:], T.rkI[:], 15, A.bitwise_and), ["rkI"], ["loI"])
+        v([ts(T.oa[:, i::16], T.loI[:], float(i), A.is_equal) for i in range(16)], ["loI"], ["oa"])
+        for c in range(8):
+            a = slice(128 * c, 128 * c + 128)
+            v(ts(T.oa[:, a], T.oa[:, a], T.v1c[:, 8 + c:9 + c], A.mult), [("oa", a.start, a.stop), "v1c"], [("oa", a.start, a.stop)])
+        p([mm(T.pC[:, 0:136], T.oa[:, 128 * c:128 * c + 128], T.th[:, 136 * c:136 * c + 136], c == 0, c == 7) for c in range(8)], ["oa", "th"], ["pC"])
+        if t == 0:
+            constants2()
+        v(tc(T.win[:, 0:136], T.pC[:, 0:136]), ["pC"], ["win"])
+        v(tc(T.g1[:], T.win[:, 0:136].indirect(T.dgt[:, 0:1])), ["win", "dgl"], ["g1"])
+        v(tt(T.lvf[:], T.win[:, 0:136].indirect(T.dgt[:, 2:3]), T.g1[:], A.subtract), ["win", "dgl", "g1"], ["lvf"])
+        v(tc(T.lv[:], T.lvf[:]), ["lvf"], ["lv"])
+        s(act(T.xg[:, 1:257], T.xw[:, 0:1025].indirect(T.lv[:])), ["xw", "lv"], [("xg", 1, 257)])
+        v(tc(T.cg[:], T.cv[:, 0:1025].indirect(T.lv[:])), ["cv", "lv"], ["cg"])
+        copies("S", T.xg, "xg", 1, 0, 128, range(11, 16))
+        copies("V", T.xg, "xg", 1, 0, 128, range(0, 11))
+        copies("S", T.xg, "xg", 129, 2048, 128, range(0, 16))
+        s(act(T.cgf[:], T.cv[:, 0:1025].indirect(T.lv[:])), ["cv", "lv"], ["cgf"])
+        s(act(T.dbf[:], T.t8[:, 0:1025].indirect(T.lv[:])), [("t8", 0, 1025), "lv"], ["dbf"])
+        if t == 0:
+            s([act(T.selb[:, 128 * k:128 * k + 128], T.idb[:], AF.Copy, 0.0, T.lmc[:, k:k + 1]) for k in range(16)], ["idb", "lmc"], ["selb"])
+        p([mm(T.pD[:, 0:256], T.cgf[:, 0:128], T.pm0[:], True, False), mm(T.pD[:, 0:256], T.cgf[:, 128:256], T.pm1[:], False, False)], ["cgf", "pm0", "pm1"], ["pD"])
+        for h in (0, 1):
+            a = slice(2048 * h, 2048 * h + 2048)
+            v(tt(T.cmp[:, a], T.sd[:, 0:2049].indirect(T.cg[:, 128 * h:128 * h + 128]), T.xr[:, a], A.is_lt),
+              [("sd", 0, 2049), "cg", ("xrS", a.start, a.start + 1), ("xrV", a.start, a.start + 1)], [("cmp", a.start, a.stop)])
+            p([mm(T.pD[:, 16 * k + 8 * h:16 * k + 8 * h + 8], T.cmp[:, a.start + k:a.stop:16], T.gik[:], False, False) for k in range(16)], [("cmp", a.start, a.stop), "gik"], ["pD"])
+        p(mm(T.pD[:, 0:256], T.one[0:1, :], T.ck[:], False, True), ["one", "ck"], ["pD"])
+        if not last:
+            for wn in W:
+                s(act(T[wn][:, 1025:1793], T.ghl[:, gha[0]:gha[1]]), [("ghl",) + gha], [(wn, 1025, 1793)])
+        v(tc(T.dbi[:, 1:257], T.dbf[:]), ["dbf"], [("dbi", 1, 257)])
+        v(tc(T.nb[:], T.pH[:, 0:8]), ["pH"], ["nb"])
+        v(ts(T.dbi[:, 1:257], T.dbi[:, 1:257], 2047, A.bitwise_and), [("dbi", 1, 257)], [("dbi", 1, 257)])
+        v([ts(T.vld[:, 8 * q:8 * q + 8], T.nb[:], T.v1c[:, q:q + 1], A.is_ge) for q in (0, 1)], ["nb", "v1c"], ["vld"])
+        tree(16)
+        v(tt(T.rz[:, 8:24], T.vld[:], T.ks[:, 16:32], A.subtract), ["vld", ("ks", 16, 32)], [("rz", 8, 24)])
+        p([mm(T.pB[:, 0:16], T.upr[:], T.rz[:, 8:24], True, False), mm(T.pB[:, 0:16], T.one[:], T.rz[:, 0:16], False, True)], ["upr", "one", "rz"], ["pB"])
+        chosen(16)
+        s(act(T.xf[:], T.ks[:, 48:64].indirect(T.ex[:])), [("ks", 48, 64), "ex"], ["xf"])
+        v(tc(T.rkI[:, 0:16], T.pB[:, 0:16]), ["pB"], ["rkI"])
+        v([ts(T.loI[:, 0:16], T.rkI[:, 0:16], 15, A.bitwise_and), ts(T.hiI[:, 0:16], T.rkI[:, 0:16], 4, A.arith_shift_right)], ["rkI"], ["loI", "hiI"])
+        v(tt(T.oa[:, 0:256], T.loI[:, 0:16].indirect(T.ex[:]), T.lane[:], A.is_equal), ["loI", "ex", "lane"], [("oa", 0, 256)])
+        v(tt(T.ob[:], T.hiI[:, 0:16].indirect(T.ex8[:]), T.ct8[:], A.is_equal), ["hiI", "ex8", "ct8"], ["ob"])
+        v([ts(T.oa[:, 256 + 128 * q:384 + 128 * q], T.oa[:, 128 * q:128 * q + 128], T.v1c[:, q:q + 1], A.mult) for q in (0, 1)], [("oa", 0, 256), "v1c"], [("oa", 256, 512)])
+        p([mm(T.pC[:, 0:64], T.oa[:, 256 + 128 * q:384 + 128 * q], T.ob[:, 64 * q:64 * q + 64], q == 0, q == 1) for q in (0, 1)], [("oa", 256, 512), "ob"], ["pC"])
+        p([mm(T.pE[:, 128 * q:128 * q + 128], T.xf[:, 128 * q:128 * q + 128], T.idF[:]) for q in (0, 1)], ["xf", "idF"], [("pE", 0, 256)])
+        v(tt(T.xe[:], T.ks[:, 48:64].indirect(T.ex[:]), T.mk[:], A.mult), [("ks", 48, 64), "ex", "mk"], ["xe"])
+        p([mm(T.pA[:, 8 * q:8 * q + 8], T.xe[:, 128 * q:128 * q + 128], T.gi16[:]) for q in (0, 1)], ["xe", "gi16"], ["pA"])
+        v(tc(T.wg[:, 0:64], T.pC[:, 0:64]), ["pC"], [("wg", 0, 64)])
+        v(lambda: V.tensor_reduce(T.thr[:, 1:2], T.ks[:, 16:32], AX.X, A.add), [("ks", 16, 32)], ["thr1"])
+        v(tc(T.gl[:], T.wg[:].indirect(T.dgt[:, 4:5])), ["wg", "dg8"], ["gl"])
+        v(tc(T.rdb[:, 0:1], T.thr[:, 1:2]), ["thr1"], ["rdb"])
+        v(tc(T.dgh[:], T.dbi[:, 0:257].indirect(T.gl[:, 0:8])), ["dbi", "gl"], ["dgh"])
+        conv(T.dgh, "dgh", 0, 8, "selh", "pF")
+        p([mm(T.pE[:, 256 + 128 * q:384 + 128 * q], T.xf[:, 128 * q:128 * q + 128], T.jF[:]) for q in (0, 1)], ["xf", "jF"], [("pE", 256, 512)])
+        if not last:
+            p(mm(T.pB[:, 64:65], T.one[:], T.rdb[:, 0:1]), ["one", "rdb"], ["pB"])
+        v(tc(T.gxs[:, gxa[0]:gxa[1]], T.xg[:, 0:257].indirect(T.gl[:, 0:8])), ["xg", "gl"], [("gxs",) + gxa])
+        send(to, T.gxl[:, gxa[0]:gxa[1]], T.gxs[:, gxa[0]:gxa[1]], [("gxs",) + gxa], "gx%d" % t)
+        s(act(T.wv[:], T.pE[:, 0:256], AF.Copy, FLAG - 1.0), ["pE"], ["wv"])
+        v(tc(T.sm[:, 112:128], T.pA[:, 0:16]), ["pA"], [("sm", 112, 128)])
+        v(ts(T.sm[:, 0:16], T.sm[:, 112:128], 0.5, A.is_lt), [("sm", 112, 128)], [("sm", 0, 16)])
+        v([tt(T.sm[:, 32:48], T.sm[:, 0:16], DUW, A.mult), tt(T.sm[:, 16:32], T.sm[:, 0:16], DUS, A.mult)], [("sm", 0, 16), "du"], [("sm", 16, 48)])
+        v(ts(T.gds[:, gda[0]:gda[1]], T.pF[:, 0:8], 1.0, A.add), ["pF"], [("gds",) + gda])
+        send(to, T.gdl[:, gda[0]:gda[1]], T.gds[:, gda[0]:gda[1]], [("gds",) + gda], "gd%d" % t)
+        ne = len(topo.engines(cores[fro], core))
+        landed(("gxl",) + gxa, "gx%d" % t, ne)
+        landed(("gdl",) + gda, "gd%d" % t, ne)
+        v([tt(T.sm[:, 48:64], T.sm[:, 32:48], T.lvf[:], A.max), tt(T.sm[:, 64:80], T.sm[:, 16:32], T.sm[:, 112:128], A.max)], [("sm", 16, 48), ("sm", 112, 128), "lvf"], [("sm", 48, 80)])
+        v(tc(T.u16s[:, 0:16], T.sm[:, 48:64]), [("sm", 48, 64)], [("u16s", 0, 16)])
+        v(lambda: V.tensor_copy(T.w1[:, 0:2064].indirect(T.u16s[:, 0:16]), T.wv[:]), ["wv", ("u16s", 0, 16)], ["w1"])
+        if last:
+            copy("Y", T.yb[:, 256:320], T.w1[0:128:16, 1:1025], [("w1", 1, 1025)], [("yb", 256, 320)])
+            copy("Y", T.yb[:, 320:384], T.pw[0:128:16, 1:1025], [("pw", 1, 1025)], [("yb", 320, 384)])
+        else:
+            jumplist(0)
+        v(tc(T.rr[:], T.pE[:, 256:512]), ["pE"], ["rr"])
+        eqdays(2)
+        scan(0)
+        scan(1)
+        alternate(dayoffsets(16), [] if last else [lambda: jumplist2(0), lambda: jump(0, (0,)), lambda: jump(0, (1,)), lambda: jumplist(1)])
+        v(lambda: V.tensor_copy(T.sd[:, 0:2320].indirect(T.u16s[:, 24:32]), T.xg[:, 129:257]), [("xg", 1, 257), ("u16s", 16, 32)], ["sd"])
+        if not last:
+            v(tc(T.smi[:, 40:41], T.pB[:, 64:65]), ["pB"], [("smi", 40, 41)])
+        v(lambda: V.tensor_copy(T.sd[:, 0:2320].indirect(T.u16s[:, 16:24]), T.xg[:, 1:129]), [("xg", 1, 257), ("u16s", 16, 32)], ["sd"])
+        copies("S", T.gxl, "gxl", gxa[0], 0, 128, range(0, 16))
+        gl = T.gdl[:, gda[0]:gda[1]]
+        s(act(T.cgf[:, 0:128], T.cw[:, 0:2049].indirect(gl)), ["cw", ("gdl",) + gda], ["cgf"])
+        if not last:
+            v(ts(T.smi[:, 41:42], T.smi[:, 40:41], 1, A.bitwise_and), [("smi", 40, 41)], [("smi", 41, 42)])
+            jumplist2(1)
+            jump(1)
+            jumplist(2)
+        v(tc(T.cg[:, 0:128], T.cw[:, 0:2049].indirect(gl)), ["cw", ("gdl",) + gda], ["cg"])
+        p(mm(T.pD[:, 0:128], T.cgf[:, 0:128], T.pmg[:], True, False), ["cgf", "pmg"], ["pD"])
+        v(tt(T.cmp[:, 0:2048], T.sd[:, 0:2049].indirect(T.cg[:, 0:128]), T.xr[:, 0:2048], A.is_lt),
+          [("sd", 0, 2049), "cg", ("xrS", 0, 1), ("xrV", 0, 1)], [("cmp", 0, 2048)])
+        p([mm(T.pD[:, 8 * k:8 * k + 8], T.cmp[:, k:2048:16], T.gik[:], False, False) for k in range(16)] +
+          [mm(T.pD[:, 0:128], T.one[0:1, :], T.ckg[:], False, True)], [("cmp", 0, 2048), "gik", "one", "ckg"], ["pD"])
+        if not last:
+            jumplist2(2)
+            jump(2)
+        else:
+            wf, pf = T.yb[:, 256:320], T.yb[:, 320:384]
+            v([ts(T.yb[:, 0:64], wf, 131072.0, A.is_ge, 1792.0, A.mult), ts(T.yb[:, 64:128], wf, 131072.0, A.is_ge, -FLAG, A.mult), ts(pf, pf, -1.0, A.add)], [("yb", 256, 384)], [("yb", 0, 128), ("yb", 320, 384)])
+            v([tt(T.yb[:, 128:192], T.yb[:, 0:64], pf, A.max), tt(T.yb[:, 192:256], T.yb[:, 64:128], wf, A.add)], [("yb", 0, 128), ("yb", 256, 384)], [("yb", 128, 256)])
+            copy("Y", T.yan[:], T.yb[:, 128:192], [("yb", 128, 192)], [])
+            copy("Y", T.yof[:], T.yb[:, 192:256], [("yb", 192, 256)], [])
+        tree(8)
+        chosen(8)
+        v(tt(T.xe[:], T.ks[:, 48:56].indirect(T.exg[:]), T.mkg[:], A.mult), [("ks", 48, 64), "exg", "mkg"], ["xe"])
+        p(mm(T.pA[:, 0:8], T.xe[:, 128:256], T.gi16[:]), ["xe", "gi16"], ["pA"])
+        p(mm(T.pE[:, 256:384], T.xe[:, 0:128], T.j16[:]), ["xe", "j16"], ["pE"])
+        if not last:
+            conv(T.t8, "t8", 1, 64, "selF", "pG")
+            v(ts(T.thr[:, 0:1], T.smi[:, 41:42], BIG, A.mult, 9.0 * BIG, A.add), [("smi", 41, 42)], ["thr"])
+        v(tc(T.sm[:, 112:120], T.pA[:, 0:8]), ["pA"], [("sm", 112, 128)])
+        v(tc(T.rr[:, 0:128], T.pE[:, 256:384]), ["pE"], ["rr"])
+        v(ts(T.sm[:, 0:8], T.sm[:, 112:120], 0.5, A.is_lt), [("sm", 112, 128)], [("sm", 0, 16)])
+        eqdays(1)
+        v(tt(T.sm[:, 16:24], T.sm[:, 0:8], T.du[:, 0:8], A.mult), [("sm", 0, 16), "du"], [("sm", 16, 48)])
+        scan(0)
+        v(tt(T.sm[:, 64:72], T.sm[:, 16:24], T.sm[:, 112:120], A.max), [("sm", 16, 48), ("sm", 112, 128)], [("sm", 48, 80)])
+        alternate(dayoffsets(8), [])
+        v(lambda a=gxa[0]: V.tensor_copy(T.sd[:, 0:2320].indirect(T.u16s[:, 16:24]), T.gxl[:, a:a + 128]), [("gxl",) + gxa, ("u16s", 16, 32)], ["sd"])
+    copy("Y", T.ys[:], T.sd[:, 1:2049], ["sd"], [])
+    finish([("ls", sent[0])])

@@ -9,11 +9,11 @@ SB = {
     "anI": (64, I), "ofI": (112, I), "snI": (48, I), "wkb": (2048, B), "xw": (1040, B), "sd": (2320, B),
     "pI": (3, I), "pp": (3, F), "tc": (8, F), "lmc": (16, F), "n512": (512, I), "kI": (256, I), "m4": (128, I),
     "id16": (128, H), "idb": (128, B), "idF": (128, F), "jF": (128, F), "j16": (128, H), "upr": (128, B),
-    "one": (128, B), "seven": (128, B), "gb16": (128, H), "gi16": (8, H), "gib": (8, B), "gik": (8, B), "pm0": (256, F), "pm1": (256, F), "pmg": (128, F),
-    "mk": (256, H), "mkg": (256, H), "lane": (256, B), "ct8": (128, B), "selh": (2048, H), "selb": (2048, B), "selF": (2048, F),
-    "ex": (16, U), "exg": (16, U), "ex8": (8, U), "dgt": (6, U), "v1c": (16, F), "smI": (1024, I), "smk": (1024, B), "du": (32, F), "lo16": (512, H),
-    "an1": (64, F), "ofE": (1792, H), "pw": (1800, F), "p2w": (1800, F), "rf16": (1024, H), "w1": (2064, F), "w2": (1800, F), "w3": (1800, F), "t8": (1032, F),
-    "fl": (1024, B), "wd": (1024, F), "p1h": (64, H), "p2h": (64, H), "p3h": (64, H), "l1": (64, U), "l2": (64, U), "l3": (64, U), "sl": (48, U), "cw": (2056, F), "cq": (2048, F),
+    "one": (128, B), "seven": (128, B), "m1k": (128, B), "gb16": (128, H), "gi16": (8, H), "gib": (8, B), "gik": (8, B), "pm0": (256, F), "pm1": (256, F), "pmg": (128, F),
+    "mk": (256, H), "mkg": (256, H), "lane": (256, B), "ct8": (128, B), "selb": (2048, B), "selF": (2048, F),
+    "ex": (16, U), "exg": (16, U), "ex8": (8, U), "dgt": (6, U), "v1c": (16, F), "smI": (1024, F), "smk": (1024, B), "du": (32, F), "lo16": (512, H),
+    "an1": (64, F), "of16": (112, H), "ofE": (1792, H), "pw": (1800, F), "p2w": (1800, F), "rf16": (1024, H), "w1": (2064, F), "w2": (1800, F), "w3": (1800, F), "t8": (1032, F),
+    "fl": (1024, B), "wd": (1024, F), "p1h": (64, H), "p2h": (64, H), "p3h": (64, H), "l1": (64, U), "l2": (64, U), "l3": (64, U), "sl": (48, U), "cw": (2056, F), "cq": (256, F), "sg": (2048, B),
     "ldI": (64, I), "lfd": (64, U), "cv": (1032, F), "cmp": (4096, B), "xr": (4096, B), "bz": (120, B), "rz": (24, B), "rkI": (64, I), "loI": (64, I), "hiI": (16, I),
     "oa": (1024, H), "ob": (128, H), "th": (1088, B), "win": (144, F), "wg": (128, F), "g1": (16, F), "lv": (16, U), "lvf": (16, F), "nb": (8, F), "vld": (16, F),
     "xg": (272, B), "cg": (256, U), "cgf": (256, F), "dbf": (256, F), "dbi": (264, I), "kb": (128, F), "ka": (128, F), "ks": (112, F), "sm": (128, F), "smi": (64, I), "u16s": (64, U),
@@ -21,7 +21,7 @@ SB = {
     "ghs": (2304, F), "ghl": (2304, F), "gxs": (512, B), "gxl": (512, B), "gds": (64, U), "gdl": (64, U),
 }
 SCRATCH = {k: ("sbuf", [128, n], d) for k, (n, d) in SB.items()}
-SCRATCH.update({"ck": ("sbuf", [1, 256], B), "ckg": ("sbuf", [1, 128], B), "cb": ("sbuf", [1, 2048], B)})
+SCRATCH.update({"ck": ("sbuf", [1, 256], B), "ckg": ("sbuf", [1, 128], B)})
 PS = ("pA", "pB", "pC", "pD", "pE", "pF", "pG", "pH")
 SCRATCH.update({k: ("psum", [128, 512], F) for k in PS})
 SEMAPHORES = ["qV", "qS", "qP", "qG", "ls"] + ["d%d" % i for i in range(11)] + ["gh%d" % t for t in range(3)] + ["gx%d" % t for t in range(RO)] + ["gd%d" % t for t in range(RO)]
@@ -167,35 +167,38 @@ def rank_program(g, core, T, topo):
     iota("pI", T.pI[:, 0:1], [[0, 1]], 0, 1)
     iota("n512", T.n512[:], [[1, 512]], 0, 0)
     iota("v1c", T.v1c[:, 0:8], [[128, 8]], 1, 1, True)
+    iota(("pw", 1025, 1794), T.pw[:, 1025:1794], [[0, 769]], 1793, 0, True)
+    iota(("p2w", 1025, 1794), T.p2w[:, 1025:1794], [[0, 769]], 1793, 0, True)
     iota("ct8", T.ct8[:], [[0, 16], [1, 8]], -256, 0, True)
     iota("ck", T.ck[:], [[-4096, 16], [0, 16]], 61440, 0, True)
     iota("ckg", T.ckg[:], [[-4096, 16], [0, 8]], 61440, 0, True)
     iota("du", T.du[:, 0:16], [[16, 16]], 2056, 0, True)
-    iota("smI", T.smI[:], [[16, 8], [1, 128]], 0, 0)
+    iota("smI", T.smI[:], [[16, 8], [1, 128]], -127, 0, True)
 
     P15, P4, PC = T.pp[:, 0:1], T.pp[:, 1:2], T.pp[:, 2:3]
+    N1, G8, K1 = T.n512[:, 0:128], T.n512[:, 0:8], T.kI[:, 0:128]
     v(ms(T.one[:], 1.0), [], ["one"])
     v([ts(T.pI[:, 1:2], T.pI[:, 0:1], 15, A.bitwise_and), ts(T.pI[:, 2:3], T.pI[:, 0:1], 4, A.arith_shift_right)], ["pI"], ["pI2"])
     v([tc(P15, T.pI[:, 1:2]), tc(P4, T.pI[:, 2:3]), tc(PC, T.pI[:, 0:1])], ["pI", "pI2"], ["pp"])
-    v([ts(T.lmc[:], T.n512[:, 0:16], P15, A.is_equal), ts(T.m4[:], T.n512[:, 0:128], 4, A.arith_shift_right), ts(T.kI[:], T.n512[:, 0:256], 15, A.bitwise_and)], ["n512", "pp"], ["lmc", "m4", "kI"])
+    v([ts(T.lmc[:], T.n512[:, 0:16], P15, A.is_equal), ts(T.m4[:], N1, 4, A.arith_shift_right), ts(T.kI[:], T.n512[:, 0:256], 15, A.bitwise_and)], ["n512", "pp"], ["lmc", "m4", "kI"])
+    v([ts(T.idb[:], N1, PC, A.is_equal), ts(T.id16[:], N1, PC, A.is_equal), ts(T.idF[:], N1, PC, A.is_equal)], ["n512", "pp"], ["idb", "id16", "idF"])
+    s([act(T.selb[:, 128 * k:128 * k + 128], T.idb[:], AF.Copy, 0.0, T.lmc[:, k:k + 1]) for k in range(16)], ["idb", "lmc"], ["selb"])
     v(ts(T.an1[:], T.anI[:], 1.0, A.add), ["anI"], ["an1"])
     v([ts(T.gb16[:], T.m4[:], P4, A.is_equal), tc(T.l1[:], T.an1[:])], ["m4", "pp", "an1"], ["gb16", "l1"])
+    v([ms(T.pw[:, 0:1], 1793.0), ms(T.p2w[:, 0:1], 1793.0)], [], [("pw", 0, 1), ("p2w", 0, 1)])
     v([ts(T.rf16[:, k::16], T.an1[:], T.lmc[:, k:k + 1], A.mult) for k in range(16)], ["an1", "lmc"], ["rf16"])
     p([mm(T.pG[:], T.gb16[:], T.rf16[:, 0:512]), mm(T.pH[:], T.gb16[:], T.rf16[:, 512:1024])], ["gb16", "rf16"], ["pG", "pH"])
-    v([ms(T.pw[:, 1025:1794], 1793.0), ms(T.pw[:, 0:1], 1793.0)], [], [("pw", 1025, 1794), ("pw", 0, 1)])
     s(act(T.pw[:, 1:513], T.pG[:]), ["pG"], [("pw", 1, 513)])
     s(act(T.pw[:, 513:1025], T.pH[:]), ["pH"], [("pw", 513, 1025)])
-    v([ts(T.ofE[:, k::16], T.ofI[:], T.lmc[:, k:k + 1], A.mult) for k in range(16)], ["ofI", "lmc"], ["ofE"])
+    v(tc(T.of16[:], T.ofI[:]), ["ofI"], ["of16"])
+    v([ts(T.ofE[:, k::16], T.of16[:], T.lmc[:, k:k + 1], A.mult) for k in range(16)], ["of16", "lmc"], ["ofE"])
     OFB = [(bank, 512 * b, min(512 * b + 512, 1792)) for b, bank in enumerate(("pA", "pB", "pC", "pD"))]
     for bank, lo, hi in OFB:
         p(mm(T[bank][:, 0:hi - lo], T.gb16[:], T.ofE[:, lo:hi]), ["gb16", "ofE"], [bank])
-    for bank, lo, hi in OFB:
-        s(act(T.w1[:, lo + 1:hi + 1], T[bank][:, 0:hi - lo]), [bank], [("w1", lo + 1, hi + 1)])
     for bank, lo, hi in OFB[:2]:
         s(act(T.wd[:, lo:hi], T[bank][:]), [bank], [("wd", lo, hi)])
-    v(ts(T.id16[:], T.n512[:, 0:128], PC, A.is_equal), ["n512", "pp"], ["id16"])
-    v([ms(T.p2w[:, 1025:1794], 1793.0), ms(T.p2w[:, 0:1], 1793.0)], [], [("p2w", 1025, 1794), ("p2w", 0, 1)])
-    v([ts(T.selh[:, 128 * k:128 * k + 128], T.id16[:], T.lmc[:, k:k + 1], A.mult) for k in range(16)], ["id16", "lmc"], ["selh"])
+    for bank, lo, hi in OFB:
+        s(act(T.w1[:, lo + 1:hi + 1], T[bank][:, 0:hi - lo]), [bank], [("w1", lo + 1, hi + 1)])
     v(lambda: V.tensor_copy(T.p2w[:, 1:1025], T.pw[:, 0:1794].indirect(T.l1[:])), ["pw", "l1"], [("p2w", 1, 1025)])
     v(tc(T.rf16[:], T.p2w[:, 1:1025]), ["p2w"], ["rf16"])
 
@@ -206,7 +209,22 @@ def rank_program(g, core, T, topo):
             fs.append(mm(o, T.id16[:], T[extra][:], False, True))
         p(fs, [(name, c0, c0 + 16 * cols), sel, "id16"] + ([extra] if extra else []), [bank])
 
-    conv(T.rf16, "rf16", 0, 64, "selh", "pF")
+    conv(T.rf16, "rf16", 0, 64, "selb", "pF")
+    v([ts(T.seven[:], N1, PC, A.is_equal, 7.0, A.mult), ts(T.m1k[:], N1, PC, A.is_equal, -1024.0, A.mult), ts(T.lo16[:], T.n512[:], 1.0, A.add)], ["n512", "pp"], ["seven", "m1k", "lo16"])
+
+    def weeks(b, second):
+        bank, c = ("pE", "pH", "pA", "pB")[b], 512 * b
+        f = [mm(T[bank][:], T.seven[:], T.wkb[:, c:c + 512], True, False), mm(T[bank][:], T.id16[:], T.lo16[:], False, not second)]
+        if second:
+            f.append(mm(T[bank][:], T.m1k[:], T.sg[:, c:c + 512], False, True))
+        p(f, ["seven", "wkb", "id16", "lo16", "m1k"] + ([("sg", c, c + 512)] if second else []), [bank])
+        if second:
+            s(act(T.cw[:, 1 + c:513 + c], T[bank][:], AF.Copy, c - 1024.0), [bank], [("cw", 1 + c, 513 + c)])
+        else:
+            s(act(T.sg[:, c:c + 512], T[bank][:], AF.Sign, c - 2048.5), [bank], [("sg", c, c + 512)])
+            if b > 1:
+                s(act(T.sg[:, c:c + 512], T.sg[:, c:c + 512], AF.Copy, c - 1024.0, -1024.0), [("sg", c, c + 512)], [("sg", c, c + 512)])
+
     zs = [("w1", 1793, 2064), ("w1", 0, 1), ("w2", 1793, 1794), ("w2", 0, 1), ("w3", 1793, 1794), ("w3", 0, 1), ("t8", 0, 1)]
     v([ms(T[n][:, a:b], 0.0) for n, a, b in zs] + [ms(T.dbi[:, 0:1], 0), ms(T.cv[:, 0:1], 1.0), ms(T.cw[:, 0:1], 1.0), ms(T.xg[:, 0:1], LOW)], [],
       zs + [("dbi", 0, 1), ("cv", 0, 1), ("cw", 0, 1), ("xg", 0, 1)])
@@ -239,47 +257,40 @@ def rank_program(g, core, T, topo):
     def jumplist2(l):
         v(ts(T[LL[l]][:], T.pF[:, 0:64], 1793.0, A.min), ["pF"], [LL[l]])
 
-    v(ts(T.idF[:], T.n512[:, 0:128], PC, A.is_equal), ["n512", "pp"], ["idF"])
     s([act(T.selF[:, 128 * k:128 * k + 128], T.idF[:], AF.Copy, 0.0, T.lmc[:, k:k + 1]) for k in range(16)], ["idF", "lmc"], ["selF"])
+    weeks(0, False)
+    weeks(1, False)
     v(tc(T.l2[:], T.pF[:, 0:64]), ["pF"], ["l2"])
     v(tc(T.p2h[:], T.pF[:, 0:64]), ["pF"], ["p2h"])
     v(lambda: V.tensor_copy(T.rf16[:], T.p2w[:, 0:1794].indirect(T.l2[:])), ["p2w", "l2"], ["rf16"])
-    conv(T.rf16, "rf16", 0, 64, "selh", "pF")
+    conv(T.rf16, "rf16", 0, 64, "selb", "pF")
     jump(0)
     addend(1)
     jump(1)
     addend(2)
+    weeks(2, False)
+    weeks(3, False)
+    weeks(0, True)
+    weeks(1, True)
     v(tc(T.l3[:], T.pF[:, 0:64]), ["pF"], ["l3"])
     v([tc(T.p3h[:], T.pF[:, 0:64]), tc(T.p1h[:], T.an1[:])], ["pF", "an1"], ["p3h", "p1h"])
     jump(2)
     conv(T.t8, "t8", 1, 64, "selF", "pG")
     v(ts(T.sl[:], T.snI[:], 1.0, A.add), ["snI"], ["sl"])
-    N1 = T.n512[:, 0:128]
-    v([ts(T.idb[:], N1, PC, A.is_equal), ts(T.seven[:], N1, PC, A.is_equal, 7.0, A.mult), ts(T.lo16[:], T.n512[:], 1.0, A.add)], ["n512", "pp"], ["idb", "seven", "lo16"])
-    v([ms(T.cb[:, 512 * b:512 * b + 512], 512.0 * b) for b in range(4)], [], ["cb"])
-    G8 = T.n512[:, 0:8]
+    for bank, c in (("pA", 1024), ("pB", 1536)):
+        v(tt(T.cw[:, 1 + c:513 + c], T[bank][:], T.sg[:, c:c + 512], A.add), [bank, ("sg", c, c + 512)], [("cw", 1 + c, 513 + c)])
     v([ts(T.gib[:], G8, P4, A.is_equal), ts(T.gi16[:], G8, P4, A.is_equal), ts(T.gik[:], G8, P4, A.is_equal, BIG, A.mult)], ["n512", "pp"], ["gib", "gi16", "gik"])
-    CB = list(enumerate(("pH", "pC", "pA", "pB")))
-    for b, bank in CB:
-        c = 512 * b
-        p([mm(T[bank][:], T.seven[:], T.wkb[:, c:c + 512], True, False), mm(T[bank][:], T.id16[:], T.lo16[:], False, False),
-           mm(T[bank][:], T.one[0:1, :], T.cb[:, c:c + 512], False, True)], ["seven", "wkb", "id16", "lo16", "one", "cb"], [bank])
-    v([ts(T.cq[:, 0:128], N1, PC, A.is_equal, -4096.0, A.mult), ts(T.cq[:, 128:256], N1, PC, A.is_gt)], ["n512", "pp"], [("cq", 0, 256)])
-    v(tt(T.upr[:], T.cq[:, 0:128], T.cq[:, 128:256], A.add), [("cq", 0, 256)], ["upr"])
+    v([ts(T.cq[:, 0:128], N1, PC, A.is_equal, -4096.0, A.mult), ts(T.cq[:, 128:256], N1, PC, A.is_gt)], ["n512", "pp"], ["cq"])
+    v(tt(T.upr[:], T.cq[:, 0:128], T.cq[:, 128:256], A.add), ["cq"], ["upr"])
     v([ms(T.bz[:, 0:56], 0.0), ms(T.rz[:, 0:8], 0.0), ms(T.wg[:, 64:128], 0.0)], [], [("bz", 0, 56), ("rz", 0, 8), ("wg", 64, 128)])
     v([ts(T.tc[:, 5:6], P4, 17.0, A.mult), ts(T.v1c[:, 8:16], T.v1c[:, 0:8], 0.5, A.mult)], ["pp", "v1c"], ["tcd", "v1c"])
     v(tt(T.tc[:, 7:8], T.tc[:, 5:6], P15, A.add), ["tcd", "pp"], ["tce"])
     v([tc(T.dgt[:, 0:1], T.tc[:, 7:8]), ts(T.dgt[:, 2:3], T.tc[:, 7:8], 1.0, A.add), tc(T.ex[:], T.n512[:, 0:16])], ["tce", "n512"], ["dgl", "ex"])
-    for b, bank in CB:
-        c = 512 * b
-        v(ts(T.cq[:, c:c + 512], T[bank][:], 2048.5, A.is_gt, -2048.0, A.mult), [bank], [("cq", c, c + 512)])
-        v(tt(T.cw[:, 1 + c:513 + c], T[bank][:], T.cq[:, c:c + 512], A.add), [bank, ("cq", c, c + 512)], [("cw", 1 + c, 513 + c)])
 
     def constants2():
-        K1 = T.kI[:, 0:128]
         v([tc(T.lane[:], T.kI[:]), ts(T.mk[:], T.kI[:], P15, A.is_equal), ts(T.mkg[:, 0:128], K1, 0.0, A.is_ge), ts(T.mkg[:, 128:256], K1, P15, A.is_equal)], ["kI", "pp"], ["lane", "mk", "mkg"])
         v([ts(T.tc[:, 0:1], P15, 16.0, A.mult), ts(T.tc[:, 1:2], P15, 8.0, A.mult), ts(T.tc[:, 3:4], P4, 8.0, A.mult), ts(T.tc[:, 2:3], P15, 8.0, A.is_ge),
-           ts(T.tc[:, 4:5], P15, -1.0, A.mult, 127.0, A.add), ts(T.smi[:, 0:16], T.n512[:, 0:16], 7, A.bitwise_and)], ["pp", "n512"], ["tc", "smi"])
+           ts(T.smi[:, 0:16], T.n512[:, 0:16], 7, A.bitwise_and)], ["pp", "n512"], ["tc", "smi"])
         v([tt(T.sm[:, 0:1], T.tc[:, 0:1], P4, A.add), tt(T.sm[:, 1:2], T.tc[:, 1:2], P4, A.add), tt(T.sm[:, 3:4], T.tc[:, 3:4], P15, A.add)], ["tc", "pp"], ["sm"])
         v([ts(T.sm[:, 2:3], T.sm[:, 0:1], 8.0, A.add), tc(T.dgt[:, 4:5], T.sm[:, 3:4])], ["sm"], ["dg8", "sm2"])
         v([ts(T.pm0[:], T.n512[:, 0:256], T.sm[:, 0:1], A.is_equal), ts(T.pm1[:], T.n512[:, 0:256], T.sm[:, 2:3], A.is_equal), ts(T.pmg[:], N1, T.sm[:, 1:2], A.is_equal)],
@@ -287,7 +298,6 @@ def rank_program(g, core, T, topo):
         v([ts(T.j16[:], N1, PC, A.add, 127.0, A.is_equal), ts(T.jF[:], N1, PC, A.add, 127.0, A.is_equal), tc(T.exg[:], T.smi[:, 0:16]), ts(T.ex8[:], G8, 2.0, A.mult, T.tc[:, 2:3], A.add),
            ts(T.du[:, 0:16], T.du[:, 0:16], P15, A.add)], ["n512", "pp", "smi", "tc", "du"], ["j16", "jF", "exg", "ex8", "du"])
         v(ts(T.du[:, 16:32], T.du[:, 0:16], -256.0, A.add), ["du"], ["du"])
-        v(ts(T.smk[:], T.smI[:], T.tc[:, 4:5], A.is_gt), ["smI", "tc"], ["smk"])
         v(ms(T.thr[:, 0:1], 9.0 * BIG), [], ["thr"])
 
     DUS, DUW = T.du[:, 0:16], T.du[:, 16:32]
@@ -352,8 +362,10 @@ def rank_program(g, core, T, topo):
         for c in range(8):
             a = slice(128 * c, 128 * c + 128)
             v(ts(T.oa[:, a], T.oa[:, a], T.v1c[:, 8 + c:9 + c], A.mult), [("oa", a.start, a.stop), "v1c"], [("oa", a.start, a.stop)])
-        p([mm(T.pC[:, 0:136], T.oa[:, 128 * c:128 * c + 128], T.th[:, 136 * c:136 * c + 136], c == 0, c == 7) for c in range(8)], ["oa", "th"], ["pC"])
+            p(mm(T.pC[:, 0:136], T.oa[:, a], T.th[:, 136 * c:136 * c + 136], c == 0, c == 7), [("oa", a.start, a.stop), "th"], ["pC"])
         if t == 0:
+            s(act(T.smI[:], T.smI[:], AF.Sign, P15), ["smI", "pp"], ["smI"])
+            s(act(T.smk[:], T.smI[:], AF.Relu), ["smI"], ["smk"])
             constants2()
         v(tc(T.win[:, 0:136], T.pC[:, 0:136]), ["pC"], ["win"])
         v(tc(T.g1[:], T.win[:, 0:136].indirect(T.dgt[:, 0:1])), ["win", "dgl"], ["g1"])
@@ -366,8 +378,6 @@ def rank_program(g, core, T, topo):
         copies("S", T.xg, "xg", 129, 2048, 128, range(0, 16))
         s(act(T.cgf[:], T.cv[:, 0:1025].indirect(T.lv[:])), ["cv", "lv"], ["cgf"])
         s(act(T.dbf[:], T.t8[:, 0:1025].indirect(T.lv[:])), [("t8", 0, 1025), "lv"], ["dbf"])
-        if t == 0:
-            s([act(T.selb[:, 128 * k:128 * k + 128], T.idb[:], AF.Copy, 0.0, T.lmc[:, k:k + 1]) for k in range(16)], ["idb", "lmc"], ["selb"])
         p([mm(T.pD[:, 0:256], T.cgf[:, 0:128], T.pm0[:], True, False), mm(T.pD[:, 0:256], T.cgf[:, 128:256], T.pm1[:], False, False)], ["cgf", "pm0", "pm1"], ["pD"])
         for h in (0, 1):
             a = slice(2048 * h, 2048 * h + 2048)
@@ -392,8 +402,8 @@ def rank_program(g, core, T, topo):
         v(tt(T.oa[:, 0:256], T.loI[:, 0:16].indirect(T.ex[:]), T.lane[:], A.is_equal), ["loI", "ex", "lane"], [("oa", 0, 256)])
         v(tt(T.ob[:], T.hiI[:, 0:16].indirect(T.ex8[:]), T.ct8[:], A.is_equal), ["hiI", "ex8", "ct8"], ["ob"])
         v([ts(T.oa[:, 256 + 128 * q:384 + 128 * q], T.oa[:, 128 * q:128 * q + 128], T.v1c[:, q:q + 1], A.mult) for q in (0, 1)], [("oa", 0, 256), "v1c"], [("oa", 256, 512)])
+        p([mm(T.pE[:, 128 * q:128 * q + 128], T.xf[:, 128 * q:128 * q + 128], T.idF[:]) for q in (0, 1)], ["xf", "idF"], ["pE"])
         p([mm(T.pC[:, 0:64], T.oa[:, 256 + 128 * q:384 + 128 * q], T.ob[:, 64 * q:64 * q + 64], q == 0, q == 1) for q in (0, 1)], [("oa", 256, 512), "ob"], ["pC"])
-        p([mm(T.pE[:, 128 * q:128 * q + 128], T.xf[:, 128 * q:128 * q + 128], T.idF[:]) for q in (0, 1)], ["xf", "idF"], [("pE", 0, 256)])
         v(tt(T.xe[:], T.ks[:, 48:64].indirect(T.ex[:]), T.mk[:], A.mult), [("ks", 48, 64), "ex", "mk"], ["xe"])
         p([mm(T.pA[:, 8 * q:8 * q + 8], T.xe[:, 128 * q:128 * q + 128], T.gi16[:]) for q in (0, 1)], ["xe", "gi16"], ["pA"])
         v(tc(T.wg[:, 0:64], T.pC[:, 0:64]), ["pC"], [("wg", 0, 64)])
@@ -401,8 +411,8 @@ def rank_program(g, core, T, topo):
         v(tc(T.gl[:], T.wg[:].indirect(T.dgt[:, 4:5])), ["wg", "dg8"], ["gl"])
         v(tc(T.rdb[:, 0:1], T.thr[:, 1:2]), ["thr1"], ["rdb"])
         v(tc(T.dgh[:], T.dbi[:, 0:257].indirect(T.gl[:, 0:8])), ["dbi", "gl"], ["dgh"])
-        conv(T.dgh, "dgh", 0, 8, "selh", "pF")
-        p([mm(T.pE[:, 256 + 128 * q:384 + 128 * q], T.xf[:, 128 * q:128 * q + 128], T.jF[:]) for q in (0, 1)], ["xf", "jF"], [("pE", 256, 512)])
+        conv(T.dgh, "dgh", 0, 8, "selb", "pF")
+        p([mm(T.pH[:, 256 + 128 * q:384 + 128 * q], T.xf[:, 128 * q:128 * q + 128], T.jF[:]) for q in (0, 1)], ["xf", "jF"], ["pH"])
         if not last:
             p(mm(T.pB[:, 64:65], T.one[:], T.rdb[:, 0:1]), ["one", "rdb"], ["pB"])
         v(tc(T.gxs[:, gxa[0]:gxa[1]], T.xg[:, 0:257].indirect(T.gl[:, 0:8])), ["xg", "gl"], [("gxs",) + gxa])
@@ -424,7 +434,7 @@ def rank_program(g, core, T, topo):
             copy("Y", T.yb[:, 320:384], T.pw[0:128:16, 1:1025], [("pw", 1, 1025)], [("yb", 320, 384)])
         else:
             jumplist(0)
-        v(tc(T.rr[:], T.pE[:, 256:512]), ["pE"], ["rr"])
+        v(tc(T.rr[:], T.pH[:, 256:512]), ["pH"], ["rr"])
         eqdays(2)
         scan(0)
         scan(1)
@@ -460,12 +470,12 @@ def rank_program(g, core, T, topo):
         chosen(8)
         v(tt(T.xe[:], T.ks[:, 48:56].indirect(T.exg[:]), T.mkg[:], A.mult), [("ks", 48, 64), "exg", "mkg"], ["xe"])
         p(mm(T.pA[:, 0:8], T.xe[:, 128:256], T.gi16[:]), ["xe", "gi16"], ["pA"])
-        p(mm(T.pE[:, 256:384], T.xe[:, 0:128], T.j16[:]), ["xe", "j16"], ["pE"])
+        p(mm(T.pH[:, 256:384], T.xe[:, 0:128], T.j16[:]), ["xe", "j16"], ["pH"])
         if not last:
             conv(T.t8, "t8", 1, 64, "selF", "pG")
             v(ts(T.thr[:, 0:1], T.smi[:, 41:42], BIG, A.mult, 9.0 * BIG, A.add), [("smi", 41, 42)], ["thr"])
         v(tc(T.sm[:, 112:120], T.pA[:, 0:8]), ["pA"], [("sm", 112, 128)])
-        v(tc(T.rr[:, 0:128], T.pE[:, 256:384]), ["pE"], ["rr"])
+        v(tc(T.rr[:, 0:128], T.pH[:, 256:384]), ["pH"], ["rr"])
         v(ts(T.sm[:, 0:8], T.sm[:, 112:120], 0.5, A.is_lt), [("sm", 112, 128)], [("sm", 0, 16)])
         eqdays(1)
         v(tt(T.sm[:, 16:24], T.sm[:, 0:8], T.du[:, 0:8], A.mult), [("sm", 0, 16), "du"], [("sm", 16, 48)])

from concourse.mybir import AluOpType as A, ActivationFunctionType as AF, AxisListType as AX

FLAG = 262144.0
BIG = 65536.0
LOW = -1073741824.0
RO = 4
F, B, H, I, U = "float32", "bfloat16", "float16", "int32", "uint16"
SB = {
    "anI": (64, I), "ofI": (112, I), "snI": (48, I), "wkb": (2048, B), "xw": (1040, B), "sd": (2320, B),
    "pI": (3, I), "pp": (3, F), "tc": (8, F), "lmc": (16, F), "n512": (512, I), "kI": (256, I), "m4": (128, I),
    "id16": (128, H), "idb": (128, B), "idF": (128, F), "jF": (128, F), "j16": (128, H), "upr": (128, B),
    "one": (128, B), "seven": (128, B), "m1k": (128, B), "gb16": (128, H), "gi16": (8, H), "gib": (8, B), "gik": (8, B), "pm0": (256, F), "pm1": (256, F), "pmg": (128, F),
    "mk": (256, H), "mkg": (256, H), "lane": (256, B), "ct8": (128, B), "selb": (2048, B), "selF": (2048, F),
    "ex": (16, U), "exg": (16, U), "ex8": (8, U), "dgt": (6, U), "v1c": (16, F), "smI": (1024, F), "smk": (1024, B), "du": (32, F), "lo16": (512, H),
    "an1": (64, F), "of16": (112, H), "ofE": (1792, H), "pw": (1800, F), "p2w": (1800, F), "rf16": (1024, H), "w1": (2064, F), "w2": (1800, F), "w3": (1800, F), "t8": (1032, F),
    "fl": (1024, B), "wd": (1024, F), "p1h": (64, H), "p2h": (64, H), "p3h": (64, H), "l1": (64, U), "l2": (64, U), "l3": (64, U), "sl": (48, U), "cw": (2056, F), "cq": (256, F), "sg": (2048, B),
    "ldI": (64, I), "lfd": (64, U), "cv": (1032, F), "cmp": (4096, B), "xr": (4096, B), "bz": (120, B), "rz": (24, B), "rkI": (64, I), "loI": (64, I), "hiI": (16, I),
    "oa": (1024, H), "ob": (128, H), "th": (1088, B), "win": (144, F), "wg": (128, F), "g1": (16, F), "lv": (16, U), "lvf": (16, F), "nb": (8, F), "vld": (16, F),
    "xg": (272, B), "cg": (256, U), "cgf": (256, F), "dbf": (256, F), "dbi": (264, I), "kb": (128, F), "ka": (128, F), "ks": (112, F), "sm": (128, F), "smi": (64, I), "u16s": (64, U),
    "rdb": (2, B), "thr": (4, F), "xe": (256, H), "xf": (256, F), "rr": (256, H), "wv": (256, F), "eq": (2048, B), "scn": (2048, B), "gl": (16, U), "dgh": (128, H), "yb": (384, F),
    "ghs": (2304, F), "ghl": (2304, F), "gxs": (512, B), "gxl": (512, B), "gds": (64, U), "gdl": (64, U),
}
SCRATCH = {k: ("sbuf", [128, n], d) for k, (n, d) in SB.items()}
SCRATCH.update({"ck": ("sbuf", [1, 256], B), "ckg": ("sbuf", [1, 128], B)})
PS = ("pA", "pB", "pC", "pD", "pE", "pF", "pG", "pH")
SCRATCH.update({k: ("psum", [128, 512], F) for k in PS})
SEMAPHORES = ["qV", "qS", "qP", "qG", "ls"] + ["d%d" % i for i in range(11)] + ["gh%d" % t for t in range(3)] + ["gx%d" % t for t in range(RO)] + ["gd%d" % t for t in range(RO)]


def layer(g, T):
    eng = {"V": g.vector, "S": g.scalar, "P": g.tensor, "G": g, "Y": g.sync}
    cnt = {"V": 0, "S": 0, "P": 0, "G": 0}
    seen = {q: {} for q in eng}
    hist = {}
    dma = [0]

    def reg(r):
        return (r, 0, 1 << 20) if isinstance(r, str) else r

    def prepare(q, reads, writes):
        best = {}
        for rs, w in ((reads, False), (writes, True)):
            for r in rs:
                name, lo, hi = reg(r)
                for e in hist.get(name, ()):
                    other = e[3] != q
                    bank = name in PS and other
                    if not (lo < e[1] and e[0] < hi) and not bank:
                        continue
                    if not (w or e[2] or bank) or (q == "P" and not other and name in PS):
                        continue
                    if seen[q].get(e[4], 0) < e[5] and (e[4] not in best or best[e[4]][5] < e[5]):
                        best[e[4]] = e
        for s in best:
            e = best[s]
            if not any(o != s and best[o][6].get(s, 0) >= e[5] for o in best):
                eng[q].wait_ge(T.sem[s], e[5])
        for e in best.values():
            for s, n in list(e[6].items()) + [(e[4], e[5])]:
                if seen[q].get(s, 0) < n:
                    seen[q][s] = n

    def record(q, sem, count, reads, writes):
        clock = dict(seen[q[0]])
        for rs, w in ((reads, False), (writes, True)):
            for r in rs:
                name, lo, hi = reg(r)
                h = hist.setdefault(name, [])
                h[:] = [e for e in h if not (lo <= e[0] and e[1] <= hi and (w or (e[3] == q and not e[2])))]
                h.append((lo, hi, w, q, sem, count, clock))

    def op(q, fns, reads, writes):
        prepare(q, reads, writes)
        for f in fns if isinstance(fns, list) else [fns]:
            f().then_inc(T.sem["q" + q], 1)
            cnt[q] += 1
        record(q, "q" + q, cnt[q], reads, writes)

    def copy(q, out, in_, reads, writes):
        prepare(q, reads, writes)
        sem = "d%d" % dma[0]
        dma[0] += 1
        eng[q].dma_start(out, in_).then_inc(T.sem[sem], 16)
        record(q + "*", sem, 16, reads, writes)

    def landed(region, sem, count):
        hist.setdefault(region[0], []).append((region[1], region[2], True, "net", sem, count, {}))

    def finish(extra):
        for q in cnt:
            if cnt[q]:
                g.wait_ge(T.sem["q" + q], cnt[q])
        for i in range(dma[0]):
            g.wait_ge(T.sem["d%d" % i], 16)
        for s, n in extra:
            g.wait_ge(T.sem[s], n)

    return op, copy, landed, prepare, finish


def alternate(a, b):
    for i in range(max(len(a), len(b))):
        for c in (a, b):
            if i < len(c):
                c[i]()


def rank_program(g, core, T, topo):
    rank = T.rank_of(core)
    if rank is None:
        return
    cores = T.cores
    N = len(cores)
    op, copy, landed, prepare, finish = layer(g, T)
    V, S, P = g.vector, g.scalar, g.tensor
    sent = [0]

    def v(f, r, w):
        op("V", f, r, w)

    def s(f, r, w):
        op("S", f, r, w)

    def p(f, r, w):
        op("P", f, r, w)

    def tc(o, i):
        return lambda: V.tensor_copy(o, i)

    def tt(o, a, b, f):
        return lambda: V.tensor_tensor(o, a, b, f)

    def ts(o, a, s1, f1, s2=None, f2=None):
        if f2 is None:
            return lambda: V.tensor_scalar(o, a, s1, None, f1)
        return lambda: V.tensor_scalar(o, a, s1, s2, f1, f2)

    def ms(o, c):
        return lambda: V.memset(o, c)

    def act(o, i, f=AF.Copy, bias=0.0, scale=1.0):
        return lambda: S.activation(o, i, f, bias=bias, scale=scale)

    def mm(o, l, r, st=True, sp=True):
        return lambda: P.matmul(o, l, r, st, sp)

    def send(dst, out, in_, reads, sem):
        d = cores[dst]
        prepare("G", reads, [])
        rid, pid = topo.addr(d, core)
        g.remote_dma(out, in_, T.sem[sem], T.sem.ls, pid, rid, topo.mask(core, d))
        sent[0] += len(topo.engines(core, d))

    def iota(name, view, pat, base, ch, fl=False):
        if fl:
            op("G", lambda: g.iota(view, pat, base, ch, allow_small_or_imprecise_dtypes=True), [], [name])
        else:
            op("G", lambda: g.iota(view, pat, base, ch), [], [name])

    v([ms(T.xw[:, 0:1], LOW), ms(T.sd[:, 0:1], 0.0)], [], [("xw", 0, 16), ("sd", 0, 16)])
    copy("Y", T.anI[:], T.an0[:], [], ["anI"])
    copy("Y", T.ofI[:], T.of0[:], [], ["ofI"])
    copy("S", T.wkb[:], T.wk[:], [], ["wkb"])
    copy("Y", T.sd[:, 1:2049], T.s0[:], [], [("sd", 1, 2049)])
    copy("Y", T.xw[:, 1:1025], T.x[:], [], [("xw", 1, 1025)])
    copy("Y", T.snI[:], T.snd[:], [], ["snI"])
    iota("pI", T.pI[:, 0:1], [[0, 1]], 0, 1)
    iota("n512", T.n512[:], [[1, 512]], 0, 0)
    iota("v1c", T.v1c[:, 0:8], [[128, 8]], 1, 1, True)
    iota(("pw", 1025, 1794), T.pw[:, 1025:1794], [[0, 769]], 1793, 0, True)
    iota(("p2w", 1025, 1794), T.p2w[:, 1025:1794], [[0, 769]], 1793, 0, True)
    iota("ct8", T.ct8[:], [[0, 16], [1, 8]], -256, 0, True)
    iota("ck", T.ck[:], [[-4096, 16], [0, 16]], 61440, 0, True)
    iota("ckg", T.ckg[:], [[-4096, 16], [0, 8]], 61440, 0, True)
    iota("du", T.du[:, 0:16], [[16, 16]], 2056, 0, True)
    iota("smI", T.smI[:], [[16, 8], [1, 128]], -127, 0, True)

    P15, P4, PC = T.pp[:, 0:1], T.pp[:, 1:2], T.pp[:, 2:3]
    N1, G8, K1 = T.n512[:, 0:128], T.n512[:, 0:8], T.kI[:, 0:128]
    v(ms(T.one[:], 1.0), [], ["one"])
    v([ts(T.pI[:, 1:2], T.pI[:, 0:1], 15, A.bitwise_and), ts(T.pI[:, 2:3], T.pI[:, 0:1], 4, A.arith_shift_right)], ["pI"], ["pI2"])
    v([tc(P15, T.pI[:, 1:2]), tc(P4, T.pI[:, 2:3]), tc(PC, T.pI[:, 0:1])], ["pI", "pI2"], ["pp"])
    v([ts(T.lmc[:], T.n512[:, 0:16], P15, A.is_equal), ts(T.m4[:], N1, 4, A.arith_shift_right), ts(T.kI[:], T.n512[:, 0:256], 15, A.bitwise_and)], ["n512", "pp"], ["lmc", "m4", "kI"])
    v([ts(T.idb[:], N1, PC, A.is_equal), ts(T.id16[:], N1, PC, A.is_equal), ts(T.idF[:], N1, PC, A.is_equal)], ["n512", "pp"], ["idb", "id16", "idF"])
    s([act(T.selb[:, 128 * k:128 * k + 128], T.idb[:], AF.Copy, 0.0, T.lmc[:, k:k + 1]) for k in range(16)], ["idb", "lmc"], ["selb"])
    v(ts(T.an1[:], T.anI[:], 1.0, A.add), ["anI"], ["an1"])
    v([ts(T.gb16[:], T.m4[:], P4, A.is_equal), tc(T.l1[:], T.an1[:])], ["m4", "pp", "an1"], ["gb16", "l1"])
    v([ms(T.pw[:, 0:1], 1793.0), ms(T.p2w[:, 0:1], 1793.0)], [], [("pw", 0, 1), ("p2w", 0, 1)])
    v([ts(T.rf16[:, k::16], T.an1[:], T.lmc[:, k:k + 1], A.mult) for k in range(16)], ["an1", "lmc"], ["rf16"])
    p([mm(T.pG[:], T.gb16[:], T.rf16[:, 0:512]), mm(T.pH[:], T.gb16[:], T.rf16[:, 512:1024])], ["gb16", "rf16"], ["pG", "pH"])
    s(act(T.pw[:, 1:513], T.pG[:]), ["pG"], [("pw", 1, 513)])
    s(act(T.pw[:, 513:1025], T.pH[:]), ["pH"], [("pw", 513, 1025)])
    v(tc(T.of16[:], T.ofI[:]), ["ofI"], ["of16"])
    v([ts(T.ofE[:, k::16], T.of16[:], T.lmc[:, k:k + 1], A.mult) for k in range(16)], ["of16", "lmc"], ["ofE"])
    OFB = [(bank, 512 * b, min(512 * b + 512, 1792)) for b, bank in enumerate(("pA", "pB", "pC", "pD"))]
    for bank, lo, hi in OFB:
        p(mm(T[bank][:, 0:hi - lo], T.gb16[:], T.ofE[:, lo:hi]), ["gb16", "ofE"], [bank])
    for bank, lo, hi in OFB[:2]:
        s(act(T.wd[:, lo:hi], T[bank][:]), [bank], [("wd", lo, hi)])
    for bank, lo, hi in OFB:
        s(act(T.w1[:, lo + 1:hi + 1], T[bank][:, 0:hi - lo]), [bank], [("w1", lo + 1, hi + 1)])
    v(lambda: V.tensor_copy(T.p2w[:, 1:1025], T.pw[:, 0:1794].indirect(T.l1[:])), ["pw", "l1"], [("p2w", 1, 1025)])
    v(tc(T.rf16[:], T.p2w[:, 1:1025]), ["p2w"], ["rf16"])

    def conv(src, name, c0, cols, sel, bank, extra=None):
        o = T[bank][:, 0:cols]
        fs = [mm(o, T[sel][:, 128 * k:128 * k + 128], src[:, c0 + k:c0 + 16 * cols:16], k == 0, k == 15 and extra is None) for k in range(16)]
        if extra is not None:
            fs.append(mm(o, T.id16[:], T[extra][:], False, True))
        p(fs, [(name, c0, c0 + 16 * cols), sel, "id16"] + ([extra] if extra else []), [bank])

    conv(T.rf16, "rf16", 0, 64, "selb", "pF")
    v([ts(T.seven[:], N1, PC, A.is_equal, 7.0, A.mult), ts(T.m1k[:], N1, PC, A.is_equal, -1024.0, A.mult), ts(T.lo16[:], T.n512[:], 1.0, A.add)], ["n512", "pp"], ["seven", "m1k", "lo16"])

    def weeks(b, second):
        bank, c = ("pE", "pH", "pA", "pB")[b], 512 * b
        f = [mm(T[bank][:], T.seven[:], T.wkb[:, c:c + 512], True, False), mm(T[bank][:], T.id16[:], T.lo16[:], False, not second)]
        if second:
            f.append(mm(T[bank][:], T.m1k[:], T.sg[:, c:c + 512], False, True))
        p(f, ["seven", "wkb", "id16", "lo16", "m1k"] + ([("sg", c, c + 512)] if second else []), [bank])
        if second:
            s(act(T.cw[:, 1 + c:513 + c], T[bank][:], AF.Copy, c - 1024.0), [bank], [("cw", 1 + c, 513 + c)])
        else:
            s(act(T.sg[:, c:c + 512], T[bank][:], AF.Sign, c - 2048.5), [bank], [("sg", c, c + 512)])
            if b > 1:
                s(act(T.sg[:, c:c + 512], T.sg[:, c:c + 512], AF.Copy, c - 1024.0, -1024.0), [("sg", c, c + 512)], [("sg", c, c + 512)])

    zs = [("w1", 1793, 2064), ("w1", 0, 1), ("w2", 1793, 1794), ("w2", 0, 1), ("w3", 1793, 1794), ("w3", 0, 1), ("t8", 0, 1)]
    v([ms(T[n][:, a:b], 0.0) for n, a, b in zs] + [ms(T.dbi[:, 0:1], 0), ms(T.cv[:, 0:1], 1.0), ms(T.cw[:, 0:1], 1.0), ms(T.xg[:, 0:1], LOW)], [],
      zs + [("dbi", 0, 1), ("cv", 0, 1), ("cw", 0, 1), ("xg", 0, 1)])
    for n in ("w2", "w3"):
        s(act(T[n][:, 1025:1537], T.pC[:]), ["pC"], [(n, 1025, 1537)])
        s(act(T[n][:, 1537:1793], T.pD[:, 0:256]), ["pD"], [(n, 1537, 1793)])
    W = ("w1", "w2", "w3")
    PH = ("p1h", "p2h", "p3h")
    LL = ("l1", "l2", "l3")

    def addend(l):
        for h in (0, 1):
            a = 512 * h
            s(act(T.wd[:, a:a + 512], T[W[l]][:, 1 + a:513 + a]), [(W[l], 1 + a, 513 + a)], [("wd", a, a + 512)])

    def jump(l, halves=(0, 1)):
        nm = "t8" if l == 2 else W[l + 1]
        for h in halves:
            a = 512 * h
            v(tt(T[nm][:, a + 1:a + 513], T[W[l]][:, 0:1794].indirect(T[LL[l]][:, 32 * h:32 * h + 32]), T.wd[:, a:a + 512], A.add),
              [(W[l], 0, 1794), LL[l], ("wd", a, a + 512)], [(nm, a + 1, a + 513)])

    def jumplist(l):
        for h in (0, 1):
            a = 512 * h
            s(act(T.fl[:, a:a + 512], T[W[l]][:, 1 + a:513 + a], AF.Relu, -2048.0, 0.015625), [(W[l], 1 + a, 513 + a)], [("fl", a, a + 512)])
        conv(T.fl, "fl", 0, 64, "selb", "pF", PH[l])
        addend(l)

    def jumplist2(l):
        v(ts(T[LL[l]][:], T.pF[:, 0:64], 1793.0, A.min), ["pF"], [LL[l]])

    s([act(T.selF[:, 128 * k:128 * k + 128], T.idF[:], AF.Copy, 0.0, T.lmc[:, k:k + 1]) for k in range(16)], ["idF", "lmc"], ["selF"])
    weeks(0, False)
    weeks(1, False)
    v(tc(T.l2[:], T.pF[:, 0:64]), ["pF"], ["l2"])
    v(tc(T.p2h[:], T.pF[:, 0:64]), ["pF"], ["p2h"])
    v(lambda: V.tensor_copy(T.rf16[:], T.p2w[:, 0:1794].indirect(T.l2[:])), ["p2w", "l2"], ["rf16"])
    conv(T.rf16, "rf16", 0, 64, "selb", "pF")
    jump(0)
    addend(1)
    jump(1)
    addend(2)
    weeks(2, False)
    weeks(3, False)
    weeks(0, True)
    weeks(1, True)
    v(tc(T.l3[:], T.pF[:, 0:64]), ["pF"], ["l3"])
    v([tc(T.p3h[:], T.pF[:, 0:64]), tc(T.p1h[:], T.an1[:])], ["pF", "an1"], ["p3h", "p1h"])
    jump(2)
    conv(T.t8, "t8", 1, 64, "selF", "pG")
    v(ts(T.sl[:], T.snI[:], 1.0, A.add), ["snI"], ["sl"])
    for bank, c in (("pA", 1024), ("pB", 1536)):
        v(tt(T.cw[:, 1 + c:513 + c], T[bank][:], T.sg[:, c:c + 512], A.add), [bank, ("sg", c, c + 512)], [("cw", 1 + c, 513 + c)])
    v([ts(T.gib[:], G8, P4, A.is_equal), ts(T.gi16[:], G8, P4, A.is_equal), ts(T.gik[:], G8, P4, A.is_equal, BIG, A.mult)], ["n512", "pp"], ["gib", "gi16", "gik"])
    v([ts(T.cq[:, 0:128], N1, PC, A.is_equal, -4096.0, A.mult), ts(T.cq[:, 128:256], N1, PC, A.is_gt)], ["n512", "pp"], ["cq"])
    v(tt(T.upr[:], T.cq[:, 0:128], T.cq[:, 128:256], A.add), ["cq"], ["upr"])
    v([ms(T.bz[:, 0:56], 0.0), ms(T.rz[:, 0:8], 0.0), ms(T.wg[:, 64:128], 0.0)], [], [("bz", 0, 56), ("rz", 0, 8), ("wg", 64, 128)])
    v([ts(T.tc[:, 5:6], P4, 17.0, A.mult), ts(T.v1c[:, 8:16], T.v1c[:, 0:8], 0.5, A.mult)], ["pp", "v1c"], ["tcd", "v1c"])
    v(tt(T.tc[:, 7:8], T.tc[:, 5:6], P15, A.add), ["tcd", "pp"], ["tce"])
    v([tc(T.dgt[:, 0:1], T.tc[:, 7:8]), ts(T.dgt[:, 2:3], T.tc[:, 7:8], 1.0, A.add), tc(T.ex[:], T.n512[:, 0:16])], ["tce", "n512"], ["dgl", "ex"])

    def constants2():
        v([tc(T.lane[:], T.kI[:]), ts(T.mk[:], T.kI[:], P15, A.is_equal), ts(T.mkg[:, 0:128], K1, 0.0, A.is_ge), ts(T.mkg[:, 128:256], K1, P15, A.is_equal)], ["kI", "pp"], ["lane", "mk", "mkg"])
        v([ts(T.tc[:, 0:1], P15, 16.0, A.mult), ts(T.tc[:, 1:2], P15, 8.0, A.mult), ts(T.tc[:, 3:4], P4, 8.0, A.mult), ts(T.tc[:, 2:3], P15, 8.0, A.is_ge),
           ts(T.smi[:, 0:16], T.n512[:, 0:16], 7, A.bitwise_and)], ["pp", "n512"], ["tc", "smi"])
        v([tt(T.sm[:, 0:1], T.tc[:, 0:1], P4, A.add), tt(T.sm[:, 1:2], T.tc[:, 1:2], P4, A.add), tt(T.sm[:, 3:4], T.tc[:, 3:4], P15, A.add)], ["tc", "pp"], ["sm"])
        v([ts(T.sm[:, 2:3], T.sm[:, 0:1], 8.0, A.add), tc(T.dgt[:, 4:5], T.sm[:, 3:4])], ["sm"], ["dg8", "sm2"])
        v([ts(T.pm0[:], T.n512[:, 0:256], T.sm[:, 0:1], A.is_equal), ts(T.pm1[:], T.n512[:, 0:256], T.sm[:, 2:3], A.is_equal), ts(T.pmg[:], N1, T.sm[:, 1:2], A.is_equal)],
          ["n512", "sm", "sm2"], ["pm0", "pm1", "pmg"])
        v([ts(T.j16[:], N1, PC, A.add, 127.0, A.is_equal), ts(T.jF[:], N1, PC, A.add, 127.0, A.is_equal), tc(T.exg[:], T.smi[:, 0:16]), ts(T.ex8[:], G8, 2.0, A.mult, T.tc[:, 2:3], A.add),
           ts(T.du[:, 0:16], T.du[:, 0:16], P15, A.add)], ["n512", "pp", "smi", "tc", "du"], ["j16", "jF", "exg", "ex8", "du"])
        v(ts(T.du[:, 16:32], T.du[:, 0:16], -256.0, A.add), ["du"], ["du"])
        v(ms(T.thr[:, 0:1], 9.0 * BIG), [], ["thr"])

    DUS, DUW = T.du[:, 0:16], T.du[:, 16:32]

    def tree(w):
        v(tc(T.kb[:, 0:8 * w], T.pD[:, 8 * w:16 * w]), ["pD"], ["kb"])
        v(tt(T.ka[:, 0:8 * w], T.pD[:, 0:8 * w], T.kb[:, 0:8 * w], A.max), ["pD", "kb"], ["ka"])
        v(tt(T.kb[:, 0:4 * w], T.ka[:, 0:4 * w], T.ka[:, 4 * w:8 * w], A.max), ["ka"], ["kb"])
        v(tt(T.ka[:, 0:2 * w], T.kb[:, 0:2 * w], T.kb[:, 2 * w:4 * w], A.max), ["kb"], ["ka"])
        v(tt(T.ks[:, 0:w], T.ka[:, 0:w], T.ka[:, w:2 * w], A.max), ["ka"], [("ks", 0, 16)])
        v([ts(T.ks[:, 16:16 + w], T.ks[:, 0:w], T.thr[:, 0:1], A.is_ge), tc(T.smi[:, 0:w], T.ks[:, 0:w])], [("ks", 0, 16), "thr"], [("ks", 16, 32), ("smi", 0, 16)])

    def chosen(w):
        v(ts(T.smi[:, 16:16 + w], T.smi[:, 0:w], 4095, A.bitwise_and), [("smi", 0, 16)], [("smi", 16, 32)])
        v(tt(T.ks[:, 48:48 + w], T.smi[:, 16:16 + w], T.ks[:, 16:16 + w], A.mult), [("smi", 16, 32), ("ks", 16, 32)], [("ks", 48, 64)])

    def eqdays(nh):
        for h in range(nh):
            v([ts(T.eq[:, b * 128:b * 128 + 128], T.rr[:, 128 * h:128 * h + 128], T.sm[:, 112 + b:113 + b], A.is_equal) for b in range(8 * h, 8 * h + 8)],
              ["rr", ("sm", 112, 128)], [("eq", 1024 * h, 1024 * h + 1024)])

    def scan(h):
        a = slice(1024 * h, 1024 * h + 1024)
        v(lambda: V.tensor_tensor_scan(T.scn[:, a], T.eq[:, a], T.smk[:], 0.0, A.max, A.mult), [("eq", a.start, a.stop), "smk"], [("scn", a.start, a.stop)])

    def dayoffsets(w):
        return [
            lambda: v(tt(T.sm[:, 80:80 + w], T.scn[:, 127:128 * w:128], T.du[:, 0:w], A.mult), ["scn", "du"], [("sm", 80, 96)]),
            lambda: v(tt(T.sm[:, 96:96 + w], T.sm[:, 64:64 + w], T.sm[:, 80:80 + w], A.max), [("sm", 64, 96)], [("sm", 96, 112)]),
            lambda: v(tc(T.u16s[:, 16:16 + w], T.sm[:, 96:96 + w]), [("sm", 96, 112)], [("u16s", 16, 32)])]

    def copies(q, src, sname, so, dst, n, ks):
        f = act if q == "S" else tc
        op(q, [f(T.xr[:, dst + k:dst + 16 * n:16], src[:, so:so + n]) for k in ks], [(sname, so, so + n)], [("xr" + q, dst, dst + 1)])

    for t in range(RO):
        last = t == RO - 1
        gxa, gda, gha = (128 * t, 128 * t + 128), (16 * t, 16 * t + 8), (768 * t, 768 * t + 768)
        to, fro = (rank + 1 + t % (N - 1)) % N, (rank - 1 - t % (N - 1)) % N
        if not last:
            s(act(T.ghs[:, gha[0]:gha[1]], T.t8[:, 0:1025].indirect(T.sl[:])), [("t8", 0, 1025), "sl"], [("ghs",) + gha])
            for d in range(1, N):
                a = gha[0] + 256 * (d - 1)
                send((rank + d) % N, T.ghl[:, a:a + 256], T.ghs[:, a:a + 256], [("ghs", a, a + 256)], "gh%d" % t)
            landed(("ghl",) + gha, "gh%d" % t, sum(len(topo.engines(cores[(rank - d) % N], core)) for d in range(1, N)))
        v(tc(T.ldI[:], T.pG[:, 0:64]), ["pG"], ["ldI"])
        v(ts(T.ldI[:], T.ldI[:], 2047, A.bitwise_and), ["ldI"], ["ldI"])
        v(ts(T.lfd[:], T.ldI[:], 1.0, A.add), ["ldI"], ["lfd"])
        for h in (0, 1):
            s(act(T.cv[:, 1 + 512 * h:513 + 512 * h], T.cw[:, 0:2049].indirect(T.lfd[:, 32 * h:32 * h + 32])), ["cw", "lfd"], [("cv", 1 + 512 * h, 513 + 512 * h)])
            v(tt(T.cmp[:, 512 * h:512 * h + 512], T.sd[:, 0:2049].indirect(T.lfd[:, 32 * h:32 * h + 32]), T.xw[:, 1 + 512 * h:513 + 512 * h], A.is_le),
              [("sd", 0, 2049), "lfd", ("xw", 1, 1025)], [("cmp", 512 * h, 512 * h + 512)])
            p([mm(T.pA[:, 8 * c:8 * c + 8], T.cmp[:, 128 * c:128 * c + 128], T.gib[:]) for c in range(4 * h, 4 * h + 4)], [("cmp", 512 * h, 512 * h + 512), "gib"], ["pA"])
        v(ts(T.bz[:, 56:120], T.pA[:, 0:64], 4.5, A.is_lt), ["pA"], [("bz", 56, 120)])
        p([mm(T.pB[:, 0:64], T.upr[:], T.bz[:, 56:120], True, False)] + [mm(T.pB[:, 0:64], T.one[:], T.bz[:, 56 - 8 * q:120 - 8 * q], False, q == 7) for q in range(1, 8)],
          ["upr", "one", "bz"], ["pB"])
        v(tc(T.rkI[:], T.pB[:, 0:64]), ["pB"], ["rkI"])
        s([act(T.th[:, c::17], T.pB[:, 0:64], AF.Sign, 16.0 * c - 4096.5, -1.0) for c in range(17)], ["pB"], ["th"])
        p([mm(T.pH[:, 0:8], T.one[:], T.bz[:, 56 + 8 * c:64 + 8 * c], c == 0, c == 7) for c in range(8)], ["one", "bz"], ["pH"])
        v(ts(T.loI[:], T.rkI[:], 15, A.bitwise_and), ["rkI"], ["loI"])
        v([ts(T.oa[:, i::16], T.loI[:], float(i), A.is_equal) for i in range(16)], ["loI"], ["oa"])
        for c in range(8):
            a = slice(128 * c, 128 * c + 128)
            v(ts(T.oa[:, a], T.oa[:, a], T.v1c[:, 8 + c:9 + c], A.mult), [("oa", a.start, a.stop), "v1c"], [("oa", a.start, a.stop)])
            p(mm(T.pC[:, 0:136], T.oa[:, a], T.th[:, 136 * c:136 * c + 136], c == 0, c == 7), [("oa", a.start, a.stop), "th"], ["pC"])
        if t == 0:
            s(act(T.smI[:], T.smI[:], AF.Sign, P15), ["smI", "pp"], ["smI"])
            s(act(T.smk[:], T.smI[:], AF.Relu), ["smI"], ["smk"])
            constants2()
        v(tc(T.win[:, 0:136], T.pC[:, 0:136]), ["pC"], ["win"])
        v(tc(T.g1[:], T.win[:, 0:136].indirect(T.dgt[:, 0:1])), ["win", "dgl"], ["g1"])
        v(tt(T.lvf[:], T.win[:, 0:136].indirect(T.dgt[:, 2:3]), T.g1[:], A.subtract), ["win", "dgl", "g1"], ["lvf"])
        v(tc(T.lv[:], T.lvf[:]), ["lvf"], ["lv"])
        s(act(T.xg[:, 1:257], T.xw[:, 0:1025].indirect(T.lv[:])), ["xw", "lv"], [("xg", 1, 257)])
        v(tc(T.cg[:], T.cv[:, 0:1025].indirect(T.lv[:])), ["cv", "lv"], ["cg"])
        copies("S", T.xg, "xg", 1, 0, 128, range(11, 16))
        copies("V", T.xg, "xg", 1, 0, 128, range(0, 11))
        copies("S", T.xg, "xg", 129, 2048, 128, range(0, 16))
        s(act(T.cgf[:], T.cv[:, 0:1025].indirect(T.lv[:])), ["cv", "lv"], ["cgf"])
        s(act(T.dbf[:], T.t8[:, 0:1025].indirect(T.lv[:])), [("t8", 0, 1025), "lv"], ["dbf"])
        p([mm(T.pD[:, 0:256], T.cgf[:, 0:128], T.pm0[:], True, False), mm(T.pD[:, 0:256], T.cgf[:, 128:256], T.pm1[:], False, False)], ["cgf", "pm0", "pm1"], ["pD"])
        for h in (0, 1):
            a = slice(2048 * h, 2048 * h + 2048)
            v(tt(T.cmp[:, a], T.sd[:, 0:2049].indirect(T.cg[:, 128 * h:128 * h + 128]), T.xr[:, a], A.is_lt),
              [("sd", 0, 2049), "cg", ("xrS", a.start, a.start + 1), ("xrV", a.start, a.start + 1)], [("cmp", a.start, a.stop)])
            p([mm(T.pD[:, 16 * k + 8 * h:16 * k + 8 * h + 8], T.cmp[:, a.start + k:a.stop:16], T.gik[:], False, False) for k in range(16)], [("cmp", a.start, a.stop), "gik"], ["pD"])
        p(mm(T.pD[:, 0:256], T.one[0:1, :], T.ck[:], False, True), ["one", "ck"], ["pD"])
        if not last:
            for wn in W:
                s(act(T[wn][:, 1025:1793], T.ghl[:, gha[0]:gha[1]]), [("ghl",) + gha], [(wn, 1025, 1793)])
        v(tc(T.dbi[:, 1:257], T.dbf[:]), ["dbf"], [("dbi", 1, 257)])
        v(tc(T.nb[:], T.pH[:, 0:8]), ["pH"], ["nb"])
        v(ts(T.dbi[:, 1:257], T.dbi[:, 1:257], 2047, A.bitwise_and), [("dbi", 1, 257)], [("dbi", 1, 257)])
        v([ts(T.vld[:, 8 * q:8 * q + 8], T.nb[:], T.v1c[:, q:q + 1], A.is_ge) for q in (0, 1)], ["nb", "v1c"], ["vld"])
        tree(16)
        v(tt(T.rz[:, 8:24], T.vld[:], T.ks[:, 16:32], A.subtract), ["vld", ("ks", 16, 32)], [("rz", 8, 24)])
        p([mm(T.pB[:, 0:16], T.upr[:], T.rz[:, 8:24], True, False), mm(T.pB[:, 0:16], T.one[:], T.rz[:, 0:16], False, True)], ["upr", "one", "rz"], ["pB"])
        chosen(16)
        s(act(T.xf[:], T.ks[:, 48:64].indirect(T.ex[:])), [("ks", 48, 64), "ex"], ["xf"])
        v(tc(T.rkI[:, 0:16], T.pB[:, 0:16]), ["pB"], ["rkI"])
        v([ts(T.loI[:, 0:16], T.rkI[:, 0:16], 15, A.bitwise_and), ts(T.hiI[:, 0:16], T.rkI[:, 0:16], 4, A.arith_shift_right)], ["rkI"], ["loI", "hiI"])
        v(tt(T.oa[:, 0:256], T.loI[:, 0:16].indirect(T.ex[:]), T.lane[:], A.is_equal), ["loI", "ex", "lane"], [("oa", 0, 256)])
        v(tt(T.ob[:], T.hiI[:, 0:16].indirect(T.ex8[:]), T.ct8[:], A.is_equal), ["hiI", "ex8", "ct8"], ["ob"])
        v([ts(T.oa[:, 256 + 128 * q:384 + 128 * q], T.oa[:, 128 * q:128 * q + 128], T.v1c[:, q:q + 1], A.mult) for q in (0, 1)], [("oa", 0, 256), "v1c"], [("oa", 256, 512)])
        p([mm(T.pE[:, 128 * q:128 * q + 128], T.xf[:, 128 * q:128 * q + 128], T.idF[:]) for q in (0, 1)], ["xf", "idF"], ["pE"])
        p([mm(T.pC[:, 0:64], T.oa[:, 256 + 128 * q:384 + 128 * q], T.ob[:, 64 * q:64 * q + 64], q == 0, q == 1) for q in (0, 1)], [("oa", 256, 512), "ob"], ["pC"])
        v(tt(T.xe[:], T.ks[:, 48:64].indirect(T.ex[:]), T.mk[:], A.mult), [("ks", 48, 64), "ex", "mk"], ["xe"])
        p([mm(T.pA[:, 8 * q:8 * q + 8], T.xe[:, 128 * q:128 * q + 128], T.gi16[:]) for q in (0, 1)], ["xe", "gi16"], ["pA"])
        v(tc(T.wg[:, 0:64], T.pC[:, 0:64]), ["pC"], [("wg", 0, 64)])
        v(lambda: V.tensor_reduce(T.thr[:, 1:2], T.ks[:, 16:32], AX.X, A.add), [("ks", 16, 32)], ["thr1"])
        v(tc(T.gl[:], T.wg[:].indirect(T.dgt[:, 4:5])), ["wg", "dg8"], ["gl"])
        v(tc(T.rdb[:, 0:1], T.thr[:, 1:2]), ["thr1"], ["rdb"])
        v(tc(T.dgh[:], T.dbi[:, 0:257].indirect(T.gl[:, 0:8])), ["dbi", "gl"], ["dgh"])
        conv(T.dgh, "dgh", 0, 8, "selb", "pF")
        p([mm(T.pH[:, 256 + 128 * q:384 + 128 * q], T.xf[:, 128 * q:128 * q + 128], T.jF[:]) for q in (0, 1)], ["xf", "jF"], ["pH"])
        if not last:
            p(mm(T.pB[:, 64:65], T.one[:], T.rdb[:, 0:1]), ["one", "rdb"], ["pB"])
        v(tc(T.gxs[:, gxa[0]:gxa[1]], T.xg[:, 0:257].indirect(T.gl[:, 0:8])), ["xg", "gl"], [("gxs",) + gxa])
        send(to, T.gxl[:, gxa[0]:gxa[1]], T.gxs[:, gxa[0]:gxa[1]], [("gxs",) + gxa], "gx%d" % t)
        s(act(T.wv[:], T.pE[:, 0:256], AF.Copy, FLAG - 1.0), ["pE"], ["wv"])
        v(tc(T.sm[:, 112:128], T.pA[:, 0:16]), ["pA"], [("sm", 112, 128)])
        v(ts(T.sm[:, 0:16], T.sm[:, 112:128], 0.5, A.is_lt), [("sm", 112, 128)], [("sm", 0, 16)])
        v([tt(T.sm[:, 32:48], T.sm[:, 0:16], DUW, A.mult), tt(T.sm[:, 16:32], T.sm[:, 0:16], DUS, A.mult)], [("sm", 0, 16), "du"], [("sm", 16, 48)])
        v(ts(T.gds[:, gda[0]:gda[1]], T.pF[:, 0:8], 1.0, A.add), ["pF"], [("gds",) + gda])
        send(to, T.gdl[:, gda[0]:gda[1]], T.gds[:, gda[0]:gda[1]], [("gds",) + gda], "gd%d" % t)
        ne = len(topo.engines(cores[fro], core))
        landed(("gxl",) + gxa, "gx%d" % t, ne)
        landed(("gdl",) + gda, "gd%d" % t, ne)
        v([tt(T.sm[:, 48:64], T.sm[:, 32:48], T.lvf[:], A.max), tt(T.sm[:, 64:80], T.sm[:, 16:32], T.sm[:, 112:128], A.max)], [("sm", 16, 48), ("sm", 112, 128), "lvf"], [("sm", 48, 80)])
        v(tc(T.u16s[:, 0:16], T.sm[:, 48:64]), [("sm", 48, 64)], [("u16s", 0, 16)])
        v(lambda: V.tensor_copy(T.w1[:, 0:2064].indirect(T.u16s[:, 0:16]), T.wv[:]), ["wv", ("u16s", 0, 16)], ["w1"])
        if last:
            copy("Y", T.yb[:, 256:320], T.w1[0:128:16, 1:1025], [("w1", 1, 1025)], [("yb", 256, 320)])
            copy("Y", T.yb[:, 320:384], T.pw[0:128:16, 1:1025], [("pw", 1, 1025)], [("yb", 320, 384)])
        else:
            jumplist(0)
        v(tc(T.rr[:], T.pH[:, 256:512]), ["pH"], ["rr"])
        eqdays(2)
        scan(0)
        scan(1)
        alternate(dayoffsets(16), [] if last else [lambda: jumplist2(0), lambda: jump(0, (0,)), lambda: jump(0, (1,)), lambda: jumplist(1)])
        v(lambda: V.tensor_copy(T.sd[:, 0:2320].indirect(T.u16s[:, 24:32]), T.xg[:, 129:257]), [("xg", 1, 257), ("u16s", 16, 32)], ["sd"])
        if not last:
            v(tc(T.smi[:, 40:41], T.pB[:, 64:65]), ["pB"], [("smi", 40, 41)])
        v(lambda: V.tensor_copy(T.sd[:, 0:2320].indirect(T.u16s[:, 16:24]), T.xg[:, 1:129]), [("xg", 1, 257), ("u16s", 16, 32)], ["sd"])
        copies("S", T.gxl, "gxl", gxa[0], 0, 128, range(0, 16))
        gl = T.gdl[:, gda[0]:gda[1]]
        s(act(T.cgf[:, 0:128], T.cw[:, 0:2049].indirect(gl)), ["cw", ("gdl",) + gda], ["cgf"])
        if not last:
            v(ts(T.smi[:, 41:42], T.smi[:, 40:41], 1, A.bitwise_and), [("smi", 40, 41)], [("smi", 41, 42)])
            jumplist2(1)
            jump(1)
            jumplist(2)
        v(tc(T.cg[:, 0:128], T.cw[:, 0:2049].indirect(gl)), ["cw", ("gdl",) + gda], ["cg"])
        p(mm(T.pD[:, 0:128], T.cgf[:, 0:128], T.pmg[:], True, False), ["cgf", "pmg"], ["pD"])
        v(tt(T.cmp[:, 0:2048], T.sd[:, 0:2049].indirect(T.cg[:, 0:128]), T.xr[:, 0:2048], A.is_lt),
          [("sd", 0, 2049), "cg", ("xrS", 0, 1), ("xrV", 0, 1)], [("cmp", 0, 2048)])
        p([mm(T.pD[:, 8 * k:8 * k + 8], T.cmp[:, k:2048:16], T.gik[:], False, False) for k in range(16)] +
          [mm(T.pD[:, 0:128], T.one[0:1, :], T.ckg[:], False, True)], [("cmp", 0, 2048), "gik", "one", "ckg"], ["pD"])
        if not last:
            jumplist2(2)
            jump(2)
        else:
            wf, pf = T.yb[:, 256:320], T.yb[:, 320:384]
            v([ts(T.yb[:, 0:64], wf, 131072.0, A.is_ge, 1792.0, A.mult), ts(T.yb[:, 64:128], wf, 131072.0, A.is_ge, -FLAG, A.mult), ts(pf, pf, -1.0, A.add)], [("yb", 256, 384)], [("yb", 0, 128), ("yb", 320, 384)])
            v([tt(T.yb[:, 128:192], T.yb[:, 0:64], pf, A.max), tt(T.yb[:, 192:256], T.yb[:, 64:128], wf, A.add)], [("yb", 0, 128), ("yb", 256, 384)], [("yb", 128, 256)])
            copy("Y", T.yan[:], T.yb[:, 128:192], [("yb", 128, 192)], [])
            copy("Y", T.yof[:], T.yb[:, 192:256], [("yb", 192, 256)], [])
        tree(8)
        chosen(8)
        v(tt(T.xe[:], T.ks[:, 48:56].indirect(T.exg[:]), T.mkg[:], A.mult), [("ks", 48, 64), "exg", "mkg"], ["xe"])
        p(mm(T.pA[:, 0:8], T.xe[:, 128:256], T.gi16[:]), ["xe", "gi16"], ["pA"])
        p(mm(T.pH[:, 256:384], T.xe[:, 0:128], T.j16[:]), ["xe", "j16"], ["pH"])
        if not last:
            conv(T.t8, "t8", 1, 64, "selF", "pG")
            v(ts(T.thr[:, 0:1], T.smi[:, 41:42], BIG, A.mult, 9.0 * BIG, A.add), [("smi", 41, 42)], ["thr"])
        v(tc(T.sm[:, 112:120], T.pA[:, 0:8]), ["pA"], [("sm", 112, 128)])
        v(tc(T.rr[:, 0:128], T.pH[:, 256:384]), ["pH"], ["rr"])
        v(ts(T.sm[:, 0:8], T.sm[:, 112:120], 0.5, A.is_lt), [("sm", 112, 128)], [("sm", 0, 16)])
        eqdays(1)
        v(tt(T.sm[:, 16:24], T.sm[:, 0:8], T.du[:, 0:8], A.mult), [("sm", 0, 16), "du"], [("sm", 16, 48)])
        scan(0)
        v(tt(T.sm[:, 64:72], T.sm[:, 16:24], T.sm[:, 112:120], A.max), [("sm", 16, 48), ("sm", 112, 128)], [("sm", 48, 80)])
        alternate(dayoffsets(8), [])
        v(lambda a=gxa[0]: V.tensor_copy(T.sd[:, 0:2320].indirect(T.u16s[:, 16:24]), T.gxl[:, a:a + 128]), [("gxl",) + gxa, ("u16s", 16, 32)], ["sd"])
    copy("Y", T.ys[:], T.sd[:, 1:2049], ["sd"], [])
    finish([("ls", sent[0])])
